import numpy as np, ml_dtypes
CORES = [2,3,42,43,82,83,122,123]
N = 8
BF = ml_dtypes.bfloat16
def gentries(a):
    return np.ascontiguousarray(a.reshape(8, 16, -1).transpose(0, 2, 1)).reshape(8, -1)
def gtable(e):
    e = np.asarray(e); return np.ascontiguousarray(e.reshape(8, -1, 16).transpose(0, 2, 1)).reshape(128, -1).astype(np.int32)
W, Q, RO, END = 3072, 2048, 3, 2 ** 20 - 1
def rise(rng, n, lo, hi, e):
    return lo + (np.sort(rng.random(n)) ** e * (hi - lo - n)).astype(np.int64) + np.arange(n)
def split(rng, w, total):
    return 1 + rng.multinomial(total - len(w), np.minimum(w * np.reciprocal(np.sum(w)), 1.0))
def families(rng, L, dev, e, total):
    u = np.exp2(dev * rng.standard_normal(L)); nb0 = split(rng, u, total); like = rng.random(L) < 0.6; like[0] = True; like[1] = False
    rest = total - int(np.sum(nb0[like])); m = L - int(np.sum(like)); nb = np.tile(nb0, (N, 1))
    for r in range(N): nb[r, ~like] = split(rng, u[~like] * np.exp2(2 * rng.standard_normal(m)), rest)
    pad = rng.integers(1, 17, (N, L)); top = np.max(16 * nb - pad, axis=0); base = []
    for l in range(L):
        t = int(top[l]); more = (0, 1, t // 16)[int(rng.integers(0, 3))] if like[l] else t // 8
        base.append(rise(rng, max(1, t + more), 0, END, e))
    return nb, pad, base
def lay(rng, nb, pad, base, mode):
    ids = np.full((N, W * 16), END, np.int64); fst = np.zeros(nb.shape, np.int64)
    for r in range(N):
        at = 0
        for l in rng.permutation(nb.shape[1]):
            b = base[l]; n = int(nb[r, l]); c = 16 * n - int(pad[r, l]); fst[r, l] = at
            if c > 0:
                if mode == 1: v = b[len(b) - c:]
                else:
                    ix = np.sort(rng.permutation(len(b))[:c])
                    if mode == 2:
                        ix[-1] = len(b) - 1
                        if c > 1: ix[0] = 0
                    v = b[ix]
                ids[r, 16 * at:16 * at + c] = v
            at += n
    return np.ascontiguousarray(ids.reshape(N, W, 16).transpose(0, 2, 1)), fst
def starts(rng, nb, fst):
    L = nb.shape[1]; f = np.tile(rng.integers(0, L, Q), (N, 1))
    f = np.where((rng.random((N, Q)) < 0.5) & (rng.random(Q) < 0.125), rng.integers(0, L, (N, Q)), f)
    u = np.where(rng.random(Q) < 0.125, rng.random((N, Q)), rng.random(Q) * (rng.random(Q) < 0.5))
    m = np.take_along_axis(nb, f, 1)
    return np.take_along_axis(fst, f, 1) + np.minimum((u * m).astype(np.int64), m - 1)
def follow(a):
    last = np.concatenate([a[..., 15, :], np.full(a.shape[:-2] + (16,), END, a.dtype)], axis=-1)
    t = np.empty(a.shape, a.dtype); t[..., 0, :] = last[..., :W]
    for i in range(1, 16): t[..., i, :] = np.where(t[..., i - 1, :] == END, END, last[..., i:i + W])
    return t
def pack(ids, st):
    a = np.stack(ids, axis=1); s = np.stack(st, axis=1)
    return {"ids": a.reshape(N, 128, W).astype(np.int32), "tops": follow(a).reshape(N, 128, W).astype(np.int32), "st": np.stack([gtable(x) for x in s])}
def setup_inputs(rng):
    ids, st = [], []
    for g in range(8):
        nb, pad, base = families(rng, int(rng.integers(12, 49)), 1.5, 1.0, W)
        a, fst = lay(rng, nb, pad, base, 0); ids.append(a); st.append(starts(rng, nb, fst))
    return pack(ids, st)
def setup_inputs_far(rng):
    ids, st = [], []; dl = np.array([0, 1, 15, 16, 17, 31, 32, 33])
    for g in range(8):
        L = 6; nb = np.tile(63 + split(rng, rng.random(L) + 0.5, W - 63 * L), (N, 1)); pad = np.tile(rng.integers(1, 17, L), (N, 1))
        base = [rise(rng, int(16 * nb[0, l] - pad[0, l]), 0, END, 1.0) for l in range(L)]
        a, fst = lay(rng, nb, pad, base, 0)
        f = rng.integers(0, L, Q); k = 33 + (rng.random(Q) * (nb[0][f] - 34)).astype(np.int64)
        d = dl[rng.integers(0, np.where(rng.random(Q) < 0.75, 4, 8), (N, Q))]; d[:, :8] = dl
        d[rng.integers(0, N, Q), np.arange(Q)] = 0
        ids.append(a); st.append(np.take_along_axis(fst, np.tile(f, (N, 1)), 1) + k - d)
    return pack(ids, st)
def setup_inputs_ends(rng):
    ids, st = [], []
    for g in range(8):
        nb, pad, base = families(rng, W // 16, 2.0, 1.0, W - 5)
        base = [rise(rng, 1, 0, END, 1.0), np.array([END - 1]), np.array([0, END - 1]), np.array([0, int(rng.integers(1, END - 1)), END - 1]), rise(rng, 15, 0, END, 1.0)] + base
        for b in base[4:]:
            b[0] = 0; b[-1] = END - 1
        nb = np.concatenate([np.ones((N, 5), np.int64), nb], axis=1); pad = np.concatenate([np.tile(np.array([16, 15, 14, 13, 1]), (N, 1)), pad], axis=1)
        a, fst = lay(rng, nb, pad, base, 2); L = nb.shape[1]
        f = np.tile(np.where(rng.random(Q) < 0.25, rng.integers(0, 5, Q), rng.integers(0, L, Q)), (N, 1))
        k = np.where(rng.random(Q) < 0.75, rng.integers(0, 3, Q), rng.integers(0, 3, (N, Q)))
        m = np.take_along_axis(nb, f, 1); s = np.take_along_axis(fst, f, 1) + np.where(k == 0, 0, np.maximum(m - k, 0))
        s[:, 0] = 0; s[:, 1] = W - 1
        ids.append(a); st.append(s)
    return pack(ids, st)
def setup_inputs_alike(rng):
    ids, st = [], []
    for g in range(8):
        L = int(rng.integers(8, 21)); nb = np.tile(split(rng, rng.random(L) + 0.2, W), (N, 1)); pad = rng.integers(1, 17, (N, L)); base = []
        for l in range(L):
            b = np.add.accumulate(rng.choice(np.array([1, 1, 1, 1, 2, 5]), int(16 * nb[0, l] - 1)))
            base.append(b - b[-1] + END - 1 if l % 2 == 0 else b - b[0] + int(rng.integers(0, END - int(b[-1] - b[0]))))
        a, fst = lay(rng, nb, pad, base, 1)
        f = rng.integers(0, L, Q); k = (rng.random(Q) * nb[0][f]).astype(np.int64)
        if g % 2 == 1:
            i = rng.integers(0, 3, Q); f = f[i]; k = k[i]
        ids.append(a); st.append(np.take_along_axis(fst, np.tile(f, (N, 1)), 1) + k)
    return pack(ids, st)
def marks(rng, n):
    k = np.sort(rng.permutation(n // 16 - 1)[:15]) + 1; i = np.concatenate([np.array([-1]), 16 * k, np.array([n])]); v = []
    for m in range(16):
        p = rise(rng, int(i[m + 1] - i[m] - 1), 65536 * m, 65536 * m + 65535, 1.0)
        if rng.random() < 0.5: p[0] = 65536 * m
        v += [p, np.array([65536 * m + 65535])]
    return np.concatenate(v)[:-1]
def runs(n):
    h = n // 16 + 1
    return np.concatenate([np.arange(65536 * m - h // 2, 65536 * m - h // 2 + h) for m in range(1, 16)] + [np.arange(END - h, END)])
def setup_inputs_cases(rng):
    ids, st = [], []; L = 6; al = np.arange(L); aq = np.arange(Q); kinds = rng.permutation(8)
    for g in range(8):
        z = int(kinds[g]); nb = np.tile(63 + split(rng, rng.random(L) + 0.5, W - 63 * L), (N, 1)); m = nb[0]
        pad = np.tile(rng.integers(1, 17, L), (N, 1)); q = rng.integers(0, N, L); add = np.zeros((N, L), np.int64)
        if z == 0:
            add = 65536 * np.stack([rng.permutation(8)[:N] for l in range(L)], axis=1); add[:, 0] = 0; add[q[0], 0] = 65536
        if z == 2:
            add[:] = 1; add[q, al] = 0
        if z == 3:
            pad[:, :3] = 1; pad[q[:3], al[:3]] = 16; pad[:, 3:] = 16; add[q[3:], al[3:]] = 2 ** 19
        base = []
        for l in range(L):
            c = int(16 * m[l] - np.min(pad[:, l]))
            if z == 0: base.append(rise(rng, c, 0, 2 ** 19, 1.0))
            elif z == 1: base.append(marks(rng, c))
            elif z == 2: base.append(rise(rng, c, 1000100, END - 1, 1.0))
            elif z == 3 and l >= 3: base.append(rise(rng, c, 0, 2 ** 18, 1.0))
            elif z == 7: base.append(runs(c * 9 // 8))
            else: base.append(rise(rng, c, 0, END, 1.0))
        a, fst = lay(rng, nb, pad, base, 0 if z == 7 else 1)
        for r in range(N):
            for l in range(L):
                s = int(fst[r, l]); x = a[r, :, s:s + int(m[l])]
                a[r, :, s:s + int(m[l])] = np.where(x < END, x + add[r, l], END)
        f = rng.integers(0, L, Q); u = rng.random(Q); k = (u * m[f]).astype(np.int64); d = np.zeros((N, Q), np.int64)
        if z == 1:
            mk = np.stack([np.flatnonzero(b % 65536 == 65535) // 16 for b in base]); k = np.where(rng.random(Q) < 0.75, mk[f, rng.integers(0, 15, Q)], k)
        if z == 3:
            e = f >= 3; k = np.where(e, m[f] - 1, 16 + (u * (m[f] - 17)).astype(np.int64))
            d = np.where(rng.random((N, Q)) < 0.5, 15, rng.integers(0, 17, (N, Q))); d[:, :Q // 4] = 15; d = np.where(e, 16, d)
            d[q[f], aq] = np.where(e, k - rng.integers(0, 8, Q), 0)
        if z == 4:
            k = 16 + (u * (m[f] - 18)).astype(np.int64); d[q[0]] = rng.integers(1, 17, Q)
        if z == 5:
            o = rng.permutation(W)[:Q]; f = np.repeat(al, m)[o]; k = (np.arange(W) - np.repeat(np.add.accumulate(m) - m, m))[o]
        if z == 6:
            f[:] = int(np.argmax(fst[0])); k = 16 + (u[0] * (m[f] - 18)).astype(np.int64); d = np.tile(rng.integers(0, 17, (N, 1)), (1, Q)); d[q[0]] = 0
        if z == 7:
            k = np.maximum(k, 1); d = rng.integers(0, 2, (N, Q))
        ids.append(a); st.append(np.take_along_axis(fst, np.tile(f, (N, 1)), 1) + k - d)
    return pack(ids, st)
def setup_inputs_spread(rng):
    ids, st = [], []
    for g in range(8):
        nb, pad, base = families(rng, int(rng.integers(4, 65)), 3.0, float(rng.choice(np.array([1.0, 3.0, 8.0]))), W)
        a, fst = lay(rng, nb, pad, base, 0); s = starts(rng, nb, fst)
        ids.append(a); st.append(np.where(rng.random(Q) < 0.25, rng.integers(0, W, (N, Q)), s))
    return pack(ids, st)
def check_inputs(d):
    bad = []
    for k, lo, hi in (("ids", 0, END), ("st", 0, W - 1)):
        if np.min(d[k]) < lo or np.max(d[k]) > hi: bad.append("range of " + k)
    a = d["ids"].astype(np.int64).reshape(N, 8, 16, W); x, y = a[:, :, :-1], a[:, :, 1:]
    if not np.all((y > x) | ((x == END) & (y == END))): bad.append("order inside a block of ids")
    x, y = a[:, :, 15, :-1], a[:, :, 0, 1:]
    if not np.all((y > x) | (x == END)): bad.append("order from block to block of ids")
    if not np.all(a[:, :, 15, W - 1] == END): bad.append("end of the last list of ids")
    if not np.array_equal(d["tops"].astype(np.int64).reshape(N, 8, 16, W), follow(a)): bad.append("tops")
    return bad
def reference(ids, tops, st):
    a = ids.astype(np.int64).reshape(N, 8, 16, W); t = tops.astype(np.int64).reshape(N, 8, 16, W)
    b = np.stack([gentries(x) for x in st]).astype(np.int64)
    cur = np.take_along_axis(a[:, :, 0], b, 2)
    hits = np.zeros((8, Q), np.int64); total = np.zeros((8, Q), np.int64)
    for rnd in range(RO):
        v = np.max(cur, axis=0); hit = (np.min(cur, axis=0) == v) & (v < END)
        hits = hits + hit; total = total + np.where(hit, v, 0); v = v + hit
        n = np.sum(np.take_along_axis(t, b[:, :, None, :], 3) < v[None, :, None, :], axis=2)
        b = b + n
        x = np.take_along_axis(a, b[:, :, None, :], 3)
        p = np.sum(x < v[None, :, None, :], axis=2)
        cur = np.take_along_axis(x, np.minimum(p, 15)[:, :, None, :], 2)[:, :, 0]
    return {"yh": np.stack([gtable(hits)] * N).astype(np.float32), "ys": np.stack([gtable(total)] * N).astype(np.float32),
            "yb": np.stack([gtable(x) for x in b]).astype(np.float32), "yc": np.stack([gtable(x) for x in cur]).astype(np.float32)}

@@ -1,0 +1,460 @@
+import numpy as np
+from concourse.bass import DstId, RemoteDMATransfer
+from concourse.mybir import AluOpType, ActivationFunctionType
+
+W, END, RO, U = 3072, 2 ** 20 - 1, 3, 4
+IDS_P = [(0, 1024), (1024, 2048), (2048, 2816), (2816, 3072)]
+TOP_P = [(0, 1024), (1024, 2048), (2048, 3072)]
+F32, BF, F16, I32, U16 = "float32", "bfloat16", "float16", "int32", "uint16"
+SB = dict(idi=(W, I32), tpi=(W, I32), xf=(W, F32), tf=(W, F32), sti=(128, I32), off=(128 * (RO + 1), U16),
+          bfl=(128 * (RO + 1), F32), xg=(512 * U * (RO + 1), F32), tg=(512 * U * RO, F32), lt1=(512 * U * RO, BF),
+          lt2=(512 * U * RO, BF), prod=(512 * U * RO, F32), pre=(64 * U * RO, F32), cmb=(64 * U * RO, F32),
+          land=(256 * U * RO, F32), tr=(224 * U * RO, F32), land8=(512 * U, F32), hh=(96 * U * RO, F16),
+          ubo=(64 * U * RO, F16), ubr=(64 * U * RO, F16), tt=(32 * U * RO, F32), s2=(256 * U, F32), res=(64 * U, F32),
+          u8=(64 * U, F32), ycs=(32 * U, F32), pint=(8, I32), ci=(8, I32), cf=(8, F32), cc=(8, F32), rowv=(256, F32),
+          rows=(512, F32), i16=(128, F16), i32x=(128, F32), i32=(128, F32), smat=(512, F16), zmat=(144, BF),
+          da=(128, BF), db=(128, BF), dm=(128, BF), gm=(32, F32), wz=(144, F32), az=(120, F32), pvs=(512 * U * 2, F32))
+SCRATCH = {k: ("sbuf", [128, n], d) for k, (n, d) in SB.items()}
+for _u in range(U):
+    SCRATCH["pp%d" % _u] = ("psum", [128, 512], F32)
+    SCRATCH["pq%d" % _u] = ("psum", [128, 512], F32)
+
+SEMAPHORES = (["cg", "cv", "ca", "ct", "lsent", "outs", "lst"]
+              + ["li%d" % i for i in range(len(IDS_P))] + ["lp%d" % i for i in range(len(TOP_P))]
+              + ["%s%d_%d" % (w, r, u) for w in ("hp", "ha", "hb") for r in range(RO) for u in range(U)]
+              + ["sm%d" % u for u in range(U)])
+CSEM = {"g": "cg", "v": "cv", "a": "ca", "t": "ct"}
+
+EST = dict(cyc=0.00104, gat=1.56, pe=0.00052, fix=0.06, afix=0.12, hop=0.1, issue=0.5, start=2.0, row=0.05,
+           byte=0.00005, first=2.0, dstart=2.0, look=0.3, stag=(9.0, 6.0, 3.0, 0.0), direct=(0, 1), split=2, fuse=1)
+OTHERS = [dict(cyc=0.00088, gat=1.2, pe=0.00045, start=1.4, row=0.03, byte=0.00004, issue=0.3),
+          dict(cyc=0.0012, gat=1.9, pe=0.0009, start=2.0, row=0.04),
+          dict(start=2.6, row=0.08, issue=0.8, hop=0.2)]
+TRIES, SEED = 3000, 1
+
+
+def tasks_of(E):
+    K = {}
+    A = AluOpType
+    CP = ActivationFunctionType.Copy
+    S = E["split"]
+
+    def add(s, name, q, dur, deps, do=None, lat=0.0, sem=None, **kw):
+        K[(s, name)] = dict(q=q, dur=dur, deps=[d if isinstance(d, tuple) else (s, d) for d in deps], do=do, lat=lat, sem=sem, **kw)
+
+    def v(n):
+        return E["fix"] + max(64, n) * E["cyc"]
+
+    def a(n):
+        return E["afix"] + n * E["cyc"]
+
+    def pe(n, k):
+        return n * E["pe"] + 0.01 * k
+
+    def rows(k, b):
+        return k * (E["row"] + b * E["byte"])
+
+    def setup(s):
+        prev = []
+        order = [("i", 0), ("st", 0), ("i", 1), ("i", 2), ("i", 3)] + [("p", k) for k in range(len(TOP_P))]
+        for kind, k in order:
+            if kind == "st":
+                q, sem, nb = "a", "lst", 512
+                do = lambda Q, T, x: [Q.dma_start(T.sti[:, :], T.st[:, :]).then_inc(T.sem.lst, 16)]
+            else:
+                lo, hi = (IDS_P if kind == "i" else TOP_P)[k]
+                q, sem, nb = ("a" if (kind, k) == ("i", 1) else "s"), "l%s%d" % (kind, k), 4 * (hi - lo)
+                do = lambda Q, T, x, kind=kind, lo=lo, hi=hi, sem=sem: [Q.dma_start(
+                    T["idi" if kind == "i" else "tpi"][:, lo:hi], T["ids" if kind == "i" else "tops"][:, lo:hi]).then_inc(T.sem[sem], 16)]
+            add(s, "ld_" + sem, q, 0.05, [], do, lat=E["dstart"], dma=True, pin=-100 + len(prev))
+            add(s, sem, "A", rows(8, nb), ["ld_" + sem] + prev[-1:], sem=(sem, 16))
+            prev.append(sem)
+        add(s, "io_p", "g", 0.15, [], lambda Q, T, x: [Q.iota(T.pint[:, 0:1], [[0, 1]], 0, 1)], pin=-3)
+        add(s, "io_r", "g", 0.6, [], lambda Q, T, x: [Q.iota(T.rowv[:, :], [[1, 256]], -64, 0, allow_small_or_imprecise_dtypes=True)], pin=-2)
+        add(s, "io_s", "g", 1.0, [], lambda Q, T, x: [Q.iota(T.rows[:, :], [[8, 4], [1, 8], [0, 16]], 0, 0, allow_small_or_imprecise_dtypes=True)], pin=-1)
+        bits = [(A.arith_shift_right, 4), (A.bitwise_and, 15), (A.bitwise_and, 31), (A.bitwise_and, 7),
+                (A.arith_shift_right, 3), (A.arith_shift_right, 6), (A.bitwise_and, 112), (A.bitwise_and, 127)]
+        for j, (op, n) in enumerate(bits):
+            add(s, "ci%d" % j, "v", v(1), ["io_p"], lambda Q, T, x, j=j, op=op, n=n: [Q.tensor_scalar(T.ci[:, j:j + 1], T.pint[:, 0:1], n, None, op)])
+        add(s, "cf", "v", v(8), ["ci%d" % j for j in range(8)], lambda Q, T, x: [Q.tensor_copy(T.cf[:, :], T.ci[:, :])])
+        cl = lambda T, c: (T[c[0]][:, c[1]:c[1] + 1] if isinstance(c, tuple) else c)
+
+        def ts(name, n, deps, out, src, s1, s2, *ops):
+            add(s, name, "v", v(n), deps, lambda Q, T, x: [Q.tensor_scalar(out(T), src(T), cl(T, s1), cl(T, s2), *ops)])
+
+        def col(name, j, deps, src, *rest):
+            ts(name, 1, deps, lambda T: T.cc[:, j:j + 1], lambda T: cl(T, src), *rest)
+        col("c_nl", 0, ["cf"], ("cf", 1), 15.0, None, A.is_lt)
+        col("c_s", 1, ["c_nl"], ("cc", 0), 2.0, -1.0, A.mult, A.add)
+        col("c_s32", 2, ["c_nl"], ("cc", 0), 2.0 / 32, -1.0 / 32, A.mult, A.add)
+        col("c_n32", 6, ["c_nl"], ("cc", 0), -2.0 / 32, 1.0 / 32, A.mult, A.add)
+        col("c_nx", 3, ["c_nl"], ("cc", 0), 16.0, ("cf", 7), A.mult, A.add)
+        col("c_w", 4, ["cf"], ("cf", 3), 16.0, ("cf", 4), A.mult, A.add)
+        col("c_ws", 5, ["cf"], ("cf", 5), -31.0, 32.0, A.mult, A.add)
+
+        def mat(name, n, deps, out, src, c, w):
+            ts(name, n, deps, out, src, c, w, *([A.is_equal] if w is None else [A.is_equal, A.mult]))
+        rv = lambda base, n: (lambda T: T.rowv[:, 64 + base:64 + base + n])
+        mat("m_g0", 8, ["cf", "io_r"], lambda T: T.gm[:, 16:32:2], lambda T: T.rowv[:, 64:192:16], ("cf", 7), 1.0 / 32)
+        mat("m_g1", 8, ["cf", "io_r"], lambda T: T.gm[:, 17:32:2], lambda T: T.rowv[:, 64:192:16], ("cf", 7), -1.0 / 32)
+        mat("m_g", 8, ["c_s32", "io_r"], lambda T: T.gm[:, 0:16:2], rv(0, 8), ("cf", 0), ("cc", 2))
+        mat("m_gn", 8, ["c_n32", "io_r"], lambda T: T.gm[:, 1:16:2], rv(0, 8), ("cf", 0), ("cc", 6))
+        mat("m_i16", 128, ["cf", "io_r"], lambda T: T.i16[:, :], rv(0, 128), ("cf", 7), None)
+        mat("m_i1", 128, ["cf", "io_r"], lambda T: T.i32[:, :], rv(0, 128), ("cf", 7), None)
+        mat("m_i32", 128, ["cf", "io_r"], lambda T: T.i32x[:, :], rv(0, 128), ("cf", 7), 32.0)
+        mat("m_s", 512, ["c_ws", "io_s"], lambda T: T.smat[:, :], lambda T: T.rows[:, :], ("cf", 2), ("cc", 5))
+        mat("m_z", 144, ["cf", "io_r"], lambda T: T.zmat[:, :], rv(-15, 144), ("cf", 6), None)
+        mat("m_da", 128, ["c_nx", "io_r"], lambda T: T.da[:, :], rv(15, 128), ("cc", 3), None)
+        mat("m_db", 128, ["c_nl", "io_r"], lambda T: T.db[:, :], rv(0, 128), ("cf", 7), ("cc", 0))
+        add(s, "m_d", "v", v(256), ["m_da", "m_db"], lambda Q, T, x: [Q.tensor_tensor(T.dm[:, :], T.da[:, :], T.db[:, :], A.subtract)])
+        mat("m_w", 144, ["c_w", "io_r"], lambda T: T.wz[:, :], rv(-12, 144), ("cc", 4), None)
+        mat("m_a", 120, ["c_s", "io_r"], lambda T: T.az[:, :], rv(-56, 120), ("cf", 0), ("cc", 1))
+        add(s, "ubz", "v", v(32 * U * RO), [], lambda Q, T, x: [Q.memset(T.ubo[96:128, :], 0.0)])
+        for k, (lo, hi) in enumerate(IDS_P):
+            ts("cvi%d" % k, hi - lo, ["li%d" % k, "c_s"], lambda T, lo=lo, hi=hi: T.xf[:, lo:hi], lambda T, lo=lo, hi=hi: T.idi[:, lo:hi], ("cc", 1), None, A.mult)
+        cvp = []
+        for k, (lo, hi) in enumerate(TOP_P):
+            for l2 in range(lo, hi, 512):
+                cvp.append("cvp%d" % l2)
+                add(s, cvp[-1], "v", v(512), ["lp%d" % k], lambda Q, T, x, l2=l2: [Q.tensor_copy(T.tf[:, l2:l2 + 512], T.tpi[:, l2:l2 + 512])])
+        add(s, "off0", "v", v(128), ["lst"], lambda Q, T, x: [Q.tensor_copy(T.off[:, 0:128], T.sti[:, :])])
+        add(s, "bfl0", "v", v(128), ["lst"], lambda Q, T, x: [Q.tensor_copy(T.bfl[:, 0:128], T.sti[:, :])])
+        return prev[-1:], ["cvi%d" % k for k in range(len(IDS_P))], cvp
+
+    def out(s, name, deps, dst, src, stag):
+        add(s, name, "s", 0.05, deps, lambda Q, T, x: [Q.dma_start(dst(T), src(T)).then_inc(T.sem.outs, 16)],
+            lat=E["dstart"] + 0.5, dma=True, out=True, stag=stag)
+
+    def unit(s, u, loaded, cvi, cvp):
+        own = (u % 2 == s)
+        gat = E["afix"] + 512 * E["cyc"] * E["gat"]
+        P = lambda T: T["pp%d" % u]
+        B = lambda T: T["pq%d" % u]
+        offs = lambda T, r: T.off[:, 128 * r + 32 * u:128 * r + 32 * u + 32]
+        bfl = lambda T, r: T.bfl[:, 128 * r + 32 * u:128 * r + 32 * u + 32]
+        l8 = lambda T, i, k=1: T.land8[:, 512 * u + 64 * i:512 * u + 64 * (i + k)]
+        tt = lambda T, r: T.tt[:, 32 * (U * r + u):32 * (U * r + u) + 32]
+        big = lambda T, nm, r, k=0, n=1: T[nm][:, 512 * (U * r + u) + k:512 * (U * r + u + 1):n]
+        rem = dict(lat=E["start"], dma=True)
+
+        def gx(r, deps):
+            add(s, "gx%d_%d" % (r, u), "a", gat, deps + cvi, lambda Q, T, x: [Q.activation(big(T, "xg", r), T.xf[:, 0:W].indirect(offs(T, r)), CP)])
+
+        def gt(r, deps):
+            add(s, "gt%d_%d" % (r, u), "a", gat, deps + cvp, lambda Q, T, x: [Q.activation(big(T, "tg", r), T.tf[:, 0:W].indirect(offs(T, r)), CP)])
+
+        def tform(name, nm, rr, gc, deps, ks):
+            add(s, name, "t", pe(256 * len(ks), len(ks)), deps, lambda Q, T, x: [Q.matmul(
+                B(T)[:, 160 + 16 * k:176 + 16 * k], big(T, nm, rr, k, 4), T.gm[:, gc:gc + 16], True, True) for k in ks])
+
+        def rnd(r, td):
+            n = lambda w: "%s%d_%d" % (w, r, u)
+            ru = U * r + u
+            ld = lambda T, i, k=1: T.land[:, 256 * ru + 64 * i:256 * ru + 64 * (i + k)]
+            pre = lambda T: T.pre[:, 64 * ru:64 * ru + 64]
+            cmb = lambda T: T.cmb[:, 64 * ru:64 * ru + 64]
+            hh = lambda T, i, k=1: T.hh[:, 96 * ru + 32 * i:96 * ru + 32 * (i + k)]
+            ubs = lambda T, nm, p: T[nm][0:p, 128 * (2 * r + u // 2):128 * (2 * r + u // 2 + 1)]
+            ub = lambda T: ubs(T, "ubo" if own else "ubr", 96)
+            tr = lambda T, lo, hi, st=1: T.tr[:, 224 * ru + lo:224 * ru + hi:st]
+            mx = lambda T: tr(T, 128, 192, 2)
+            cur = lambda T: B(T)[:, 160:224]
+            direct = r == 0 and u in E["direct"]
+            iss = E["issue"] + (E["first"] if r == 0 and u == (0 if 0 in E["direct"] else s) else 0.0)
+            if own:
+                add(s, n("Tc"), "v", v(64), td, lambda Q, T, x: [Q.tensor_scalar(l8(T, x["rank"]) if direct else pre(T), cur(T), -(END - 1) / 32.0, None, A.max)])
+                if direct:
+                    add(s, n("s1"), "g", iss, [n("Tc")], lambda Q, T, x: hop1(x, l8(T, x["rank"]), l8(T, x["rank"]), u, n("ha"), False), **rem)
+                    add(s, n("w1"), "A", rows(48, 256), [n("s1")])
+                    add(s, n("ha"), None, 0, [n("w1"), (1 - s, n("w1")), (1 - s, n("w1b"))], sem=(n("ha"), "all"))
+                    add(s, n("x8"), "v", v(512), [n("ha"), n("Tc")], lambda Q, T, x: [Q.tensor_tensor(ld(T, 0, 4), l8(T, 0, 4), l8(T, 4, 4), A.max)])
+                else:
+                    add(s, n("s0"), "g", iss, [n("Tc")], lambda Q, T, x: tosib(x, pre(T), n("hp")), **rem)
+                    add(s, n("w0"), "B", rows(16, 256), [n("s0")] + loaded)
+                    add(s, n("ha"), None, 0, [(1 - s, n("w1")), (1 - s, n("w1b"))], sem=(n("ha"), None))
+                add(s, n("xa"), "v", v(256), [n("x8" if direct else "ha")], lambda Q, T, x: [Q.tensor_tensor(tr(T, 0, 128), ld(T, 0, 2), ld(T, 2, 2), A.max)])
+                add(s, n("xb"), "v", v(128), [n("xa")], lambda Q, T, x: [Q.tensor_tensor(tr(T, 128, 192), tr(T, 0, 64), tr(T, 64, 128), A.max)])
+                add(s, n("hi"), "v", v(32), [n("xb")], lambda Q, T, x: [Q.tensor_copy(hh(T, 0), mx(T))])
+                add(s, n("df"), "v", v(64), [n("xb")], lambda Q, T, x: [Q.tensor_tensor(tr(T, 192, 224), mx(T), tr(T, 129, 192, 2), A.add)])
+                add(s, n("lo"), "v", v(64), [n("hi")], lambda Q, T, x: [Q.tensor_tensor(hh(T, 1), mx(T), hh(T, 0), A.subtract)])
+                add(s, n("ht"), "v", v(32), [n("df")], lambda Q, T, x: [Q.tensor_scalar(hh(T, 2), tr(T, 192, 224), 0.0, None, A.is_le)])
+                add(s, n("tt"), "v", v(64), [n("ht")], lambda Q, T, x: [Q.tensor_tensor(tt(T, r), mx(T), hh(T, 2), A.mult)])
+                if r:
+                    add(s, n("ts"), "v", v(64), [n("tt"), ("ts%d_%d" if r > 1 else "tt%d_%d") % (r - 1, u)], lambda Q, T, x: [Q.tensor_tensor(tt(T, r), tt(T, r), tt(T, r - 1), A.add)])
+                add(s, n("U"), "t", pe(128, 1), [n("lo"), n("ht"), n("Tc"), "m_i16"], lambda Q, T, x: [Q.matmul(B(T)[0:96, 0:128], hh(T, 0, 3), T.i16[:, :], True, True)])
+                add(s, n("Uc"), "v", v(128), [n("U")], lambda Q, T, x: [Q.tensor_copy(ub(T), B(T)[0:96, 0:128])])
+                add(s, n("s2"), "g", E["issue"], [n("Uc"), "ubz"], lambda Q, T, x: tosib(x, ubs(T, "ubo", 128), n("hb"), ubs(T, "ubr", 128)), **rem)
+                add(s, n("w2"), "B", rows(16, 256), [n("s2")])
+                hd = [n("Uc")]
+            else:
+                if direct:
+                    add(s, n("Tc"), "v", v(64), td, lambda Q, T, x: [Q.tensor_copy(l8(T, x["rank"]), cur(T))])
+                    add(s, n("s1"), "g", iss, [n("Tc")], lambda Q, T, x: hop1(x, l8(T, x["rank"]), l8(T, x["rank"]), u, n("ha"), True), **rem)
+                else:
+                    add(s, n("hp"), None, 0, [(1 - s, n("w0"))], sem=(n("hp"), None))
+                    add(s, n("Tc"), "v", v(64), td + [n("hp")], lambda Q, T, x: [Q.tensor_tensor(cmb(T), pre(T), cur(T), A.max)])
+                    add(s, n("s1"), "g", E["issue"], [n("Tc")], lambda Q, T, x: hop1(x, cmb(T), ld(T, x["slot"]), u, n("ha"), True), **rem)
+                add(s, n("w1"), "A", rows(48, 256), [n("s1")])
+                add(s, n("w1b"), "B", rows(16, 256), [n("s1")] + loaded)
+                add(s, n("hb"), None, 0, [(1 - s, n("w2"))], sem=(n("hb"), None))
+                hd = [n("hb"), n("Tc")]
+            add(s, n("B"), "t", pe(512, 4), hd + ["m_s"], lambda Q, T, x: [Q.matmul(
+                P(T)[:, k:512:4], T.smat[0:96, 128 * k:128 * k + 128], ub(T), True, True) for k in range(4)])
+            add(s, n("Nb"), "t", pe(256, 1), [n("B"), "m_i1", ("ba%d_%d" % (r - 1, u) if r else "bfl0")],
+                lambda Q, T, x: [Q.matmul(B(T)[:, 128:160], T.i32[:, :], bfl(T, r), True, False)], same=[n("B")])
+            last = n("Nb")
+            for h in range(S):
+                add(s, n("c1" + "ab"[h]), "v", v(512 // S), [n("B"), n("gt")], lambda Q, T, x, h=h: [Q.tensor_tensor(big(T, "lt1", r, h, S), big(T, "tg", r, h, S), P(T)[:, h:512:S], A.is_lt)])
+                add(s, n("N" + "xy"[h]), "t", pe(1024 // S, 16 // S), [n("c1" + "ab"[h]), last, "m_z"], lambda Q, T, x, h=h: [Q.matmul(
+                    B(T)[:, 128:160], T.zmat[:, 15 - k:143 - k], big(T, "lt1", r, k, 16), False, k == 15) for k in range(h, 16, S)], same=[last])
+                last = n("N" + "xy"[h])
+            add(s, n("bo"), "v", v(32), [last], lambda Q, T, x: [Q.tensor_copy(offs(T, r + 1), B(T)[:, 128:160])])
+            gx(r + 1, [n("bo")])
+            add(s, n("ba"), "a", a(32), [n("bo")], lambda Q, T, x: [Q.activation(bfl(T, r + 1), B(T)[:, 128:160], CP)])
+            if r + 1 < RO:
+                gt(r + 1, [n("bo")])
+            if E["fuse"]:
+                add(s, n("pc"), "a", a(512), [n("c1" + "ab"[h]) for h in range(S)], lambda Q, T, x: [Q.activation(big(T, "pvs", r % 2), P(T)[:, :], CP)])
+                add(s, n("c2"), "v", E["fix"] + 512 * E["cyc"] * E["gat"], [n("bo"), n("pc")], lambda Q, T, x: [Q.tensor_tensor(big(T, "lt2", r), T.xf[:, 0:W].indirect(offs(T, r + 1)), big(T, "pvs", r % 2), A.is_lt)])
+            else:
+                add(s, n("c2"), "v", v(512), ["gx%d_%d" % (r + 1, u), n("B")], lambda Q, T, x: [Q.tensor_tensor(big(T, "lt2", r), big(T, "xg", r + 1), P(T)[:, :], A.is_lt)])
+            add(s, n("S"), "t", pe(512, 1), [n("c2"), "m_d"], lambda Q, T, x: [Q.matmul(P(T)[:, :], T.dm[:, :], big(T, "lt2", r), True, True)])
+            td = []
+            for h in range(S):
+                add(s, n("mu" + "ab"[h]), "v", v(512 // S), [n("S"), "gx%d_%d" % (r + 1, u)], lambda Q, T, x, h=h: [Q.tensor_tensor(big(T, "prod", r, h, S), big(T, "xg", r + 1, h, S), P(T)[:, h:512:S], A.mult)])
+                if r + 1 < RO:
+                    td.append(n("T" + "ab"[h]))
+                    tform(td[-1], "prod", r, 0, [n("mu" + "ab"[h]), n("ba"), "m_g", "m_gn"], list(range(h, 4, S)))
+            return td
+
+        gx(0, ["off0"])
+        gt(0, ["off0"])
+        td = ["T_%d" % u]
+        tform(td[0], "xg", 0, 16, ["gx0_%d" % u, "m_g0", "m_g1"], [0, 1, 2, 3])
+        for r in range(RO):
+            td = rnd(r, td)
+        n = lambda w: "%s%d_%d" % (w, RO - 1, u)
+        rs = lambda T, i, k=1: T.res[:, 64 * u + 32 * i:64 * u + 32 * (i + k)]
+        free = [n("ba")]
+        if own:
+            add(s, n("HA"), "t", pe(896, 4), [n("ba"), n("ts"), "m_i32", "m_i16"], lambda Q, T, x: [
+                Q.matmul(B(T)[0:32, 256:384], tt(T, RO - 1), T.i32x[:, :], True, True)] + [
+                Q.matmul(B(T)[0:32, 384:512], T.hh[:, 96 * (U * r + u) + 64:96 * (U * r + u) + 96], T.i16[:, :], r == 0, r == RO - 1) for r in range(RO)])
+            add(s, n("Hc"), "a", a(256), [n("HA")], lambda Q, T, x: [Q.activation(T.s2[0:32, 256 * u:256 * u + 256], B(T)[0:32, 256:512], CP)])
+            add(s, n("HB"), "t", pe(1024, 4), [n("Hc"), "m_w"], lambda Q, T, x: [Q.matmul(
+                B(T)[:, 192:256], T.wz[0:32, 12 - 4 * k:140 - 4 * k], T.s2[0:32, 256 * u + k:256 * u + 256:4], k == 0, k == 3) for k in range(4)])
+            add(s, n("Hd"), "a", a(64), [n("HB")], lambda Q, T, x: [Q.activation(rs(T, 0, 2), B(T)[:, 192:256], CP)])
+            add(s, n("s3"), "g", E["issue"], [n("Hd")], lambda Q, T, x: tosib(x, rs(T, 0, 2), "sm%d" % u), **rem)
+            add(s, n("w3"), "B", rows(16, 256), [n("s3")])
+            d = free = [n("Hd")]
+        else:
+            add(s, "sm%d" % u, None, 0, [(1 - s, n("w3"))], sem=("sm%d" % u, None))
+            d = ["sm%d" % u]
+        out(s, n("os"), d, lambda T: T.ys[:, 32 * u:32 * u + 32], lambda T: rs(T, 0), E["stag"][u])
+        out(s, n("oh"), d, lambda T: T.yh[:, 32 * u:32 * u + 32], lambda T: rs(T, 1), E["stag"][u])
+        last = []
+        for h in range(S):
+            add(s, n("FA" + "ab"[h]), "t", pe(2048 // S, 8 // S), [n("mu" + "ab"[h]), "m_a"] + free + last, lambda Q, T, x, h=h: [Q.matmul(
+                B(T)[0:64, 0:64], T.az[:, 56 - 8 * k:120 - 8 * k], big(T, "prod", RO - 1, k, 8), k == 0, k == 7) for k in range(h, 8, S)], same=last)
+            last = [n("FA" + "ab"[h])]
+        add(s, n("Fc"), "a", a(64), last, lambda Q, T, x: [Q.activation(T.u8[0:64, 64 * u:64 * u + 64], B(T)[0:64, 0:64], CP)])
+        add(s, n("FB"), "t", pe(512, 2), [n("Fc"), "m_w"], lambda Q, T, x: [Q.matmul(
+            B(T)[:, 64:96], T.wz[0:64, 12 - 8 * k:140 - 8 * k], T.u8[0:64, 64 * u + k:64 * u + 64:2], k == 0, k == 1) for k in range(2)])
+        add(s, n("Fd"), "a", a(32), [n("FB")], lambda Q, T, x: [Q.activation(T.ycs[:, 32 * u:32 * u + 32], B(T)[:, 64:96], CP)])
+        out(s, n("oc"), [n("Fd")], lambda T: T.yc[:, 32 * u:32 * u + 32], lambda T: T.ycs[:, 32 * u:32 * u + 32], E["stag"][u])
+
+    for s in (0, 1):
+        pr = setup(s)
+        for u in range(U):
+            unit(s, u, *pr)
+        out(s, "ob", ["ba%d_%d" % (RO - 1, u) for u in range(U)], lambda T: T.yb[:, :], lambda T: T.bfl[:, 128 * RO:128 * RO + 128], 0.0)
+    for t in K.values():
+        t["gap"] = t["lat"] + (E["hop"] if t["do"] and not t.get("dma") or t["sem"] else 0.0)
+    return K
+
+
+def dst_id(topo, c):
+    ad = topo.addr(c)
+    return DstId(rid=ad[0], pnc=ad[1])
+
+
+def hop1(x, src, dst, u, sem, sib):
+    T, topo = x["T"], x["topo"]
+    n = len(x["pairs"])
+    far = [x["pairs"][(x["slot"] + k) % n][u % 2] for k in range(1, n)]
+    trs = [RemoteDMATransfer(dst_ids=[dst_id(topo, d) for d in far], dma_engine_mask=x["moff"], remote_sem=T.sem[sem],
+                             srcs=[src], dsts=[dst for d in far])]
+    x["sent"][0] += x["noff"]
+    if sib:
+        trs.append(RemoteDMATransfer(dst_ids=[dst_id(topo, x["sib"])], dma_engine_mask=x["mon"], remote_sem=T.sem[sem],
+                                     srcs=[src], dsts=[dst]))
+        x["sent"][0] += x["non"]
+    return [x["g"].remote_dma_fused(trs, local_sem=T.sem.lsent)]
+
+
+def tosib(x, src, sem, dst=None):
+    ad = x["topo"].addr(x["sib"])
+    x["sent"][0] += x["non"]
+    return [x["g"].remote_dma(src if dst is None else dst, src, x["T"].sem[sem], x["T"].sem.lsent, ad[1], ad[0], x["mon"])]
+
+
+def plan(K, E, prio):
+    kids = {k: [] for k in K}
+    for k, t in K.items():
+        for d in t["deps"]:
+            kids[d].append(k)
+    tail = {}
+
+    def way(k):
+        if k not in tail:
+            tail[k] = K[k]["dur"] + K[k]["gap"] + max([way(c) for c in kids[k]] + [K[k].get("stag", 0.0)])
+        return tail[k]
+    key = {k: (K[k].get("pin", 0), -way(k) - prio.get(k, 0.0)) for k in K}
+    left = {k: len(K[k]["deps"]) for k in K}
+    ready = {}
+    for k in K:
+        if left[k] == 0:
+            ready.setdefault((k[0], K[k]["q"]), []).append(k)
+    rt = {k: 0.0 for k in K}
+    free, order, end = {}, [], 0.0
+    while ready:
+        best = None
+        for q, l in ready.items():
+            f = free.get(q, 0.0) if q[1] else 0.0
+            m = max(min(rt[k] for k in l), f)
+            if best is None or m < best[0]:
+                best = (m, q, f)
+        m, q, f = best
+        k0 = min([k for k in ready[q] if rt[k] <= m], key=key.get)
+        look = 0.0 if q[1] in ("A", "B") else max(0.0, E["look"] * K[k0]["dur"] + prio.get((k0, "w"), 0.0))
+        k1 = min([k for k in ready[q] if rt[k] <= m + look], key=key.get)
+        ready[q].remove(k1)
+        if not ready[q]:
+            del ready[q]
+        order.append(k1)
+        e = max(rt[k1], f) + K[k1]["dur"]
+        if q[1]:
+            free[q] = e
+        e += K[k1]["gap"]
+        end = max(end, e)
+        for c in kids[k1]:
+            rt[c] = max(rt[c], e)
+            left[c] -= 1
+            if left[c] == 0:
+                ready.setdefault((c[0], K[c]["q"]), []).append(c)
+    return order, end
+
+
+def replay(K, order):
+    free, fin = {}, {}
+    for k in order:
+        t = K[k]
+        st = max([fin[d] for d in t["deps"]] + [free.get((k[0], t["q"]), 0.0)])
+        if t["q"]:
+            free[(k[0], t["q"])] = st + t["dur"]
+        fin[k] = st + t["dur"] + t["gap"]
+    return max(fin.values()), fin
+
+
+def search(E, tries, seed):
+    K = tasks_of(E)
+    KO = [tasks_of(dict(E, **o)) for o in OTHERS]
+    names = [k for k in K if K[k]["do"] and K[k]["q"] in "vatg" and k[1][-2:-1] == "_"]
+    rng = np.random.RandomState(seed)
+
+    def cost(p):
+        o, e = plan(K, E, p)
+        return e + sum(replay(k2, o)[0] for k2 in KO), o
+    prio = {}
+    best, order = cost(prio)
+    for it in range(tries):
+        p = dict(prio)
+        for j in range(int(rng.randint(1, 4))):
+            k = names[int(rng.randint(len(names)))]
+            z = rng.rand()
+            if z < 0.3:
+                dl = float(rng.randn() * 2.0)
+                for k2 in names:
+                    if k2[0] == k[0] and k2[1][-3:] == k[1][-3:]:
+                        p[k2] = p.get(k2, 0.0) + dl
+            elif z < 0.5:
+                p[(k, "w")] = float(rng.rand() * 1.5 - 0.3)
+            else:
+                p[k] = p.get(k, 0.0) + float(rng.randn() * 3.0)
+        c, o = cost(p)
+        if c <= best:
+            best, order, prio = c, o, p
+    return K, order, best
+
+
+MEMO = {}
+
+
+def rank_program(g, core, T, topo):
+    rank = T.rank_of(core)
+    if rank is None:
+        return
+    if "plan" not in MEMO:
+        MEMO["K"], MEMO["plan"], MEMO["cost"] = search(EST, TRIES, SEED)
+    K = MEMO["K"]
+    chips = []
+    for c in T.cores:
+        if topo.chip(c) not in chips:
+            chips.append(topo.chip(c))
+    pairs = [[c for c in T.cores if topo.chip(c) == ch] for ch in chips]
+    mine = [p for p in pairs if core in p][0]
+    side = mine.index(core)
+    sib = mine[1 - side]
+    moff = -1
+    for c in T.cores:
+        if c not in mine:
+            moff &= topo.mask(core, c)
+    mon = topo.mask(core, sib) & ~moff
+    noff, non = bin(moff).count("1"), bin(mon).count("1")
+    x = dict(g=g, T=T, topo=topo, pairs=pairs, sib=sib, moff=moff, mon=mon, noff=noff, non=non, sent=[0],
+             rank=rank, slot=pairs.index(mine))
+    QS = {"g": g, "v": g.vector, "a": g.scalar, "t": g.tensor, "s": g.sync}
+    count = {q: 0 for q in CSEM}
+    known = {q: {} for q in QS}
+    done = {}
+    outs = [0]
+    for k in MEMO["plan"]:
+        t = K[k]
+        if k[0] != side:
+            continue
+        if t["sem"]:
+            name, val = t["sem"]
+            if val == "all":
+                val = (len(T.cores) - 2) * noff + non
+            elif val is None:
+                val = (len(pairs) - 1) * noff + non if name.startswith("ha") else non
+            done[k] = (name, val, {})
+            continue
+        if t["do"] is None:
+            continue
+        q = t["q"]
+        need = {}
+        for d in t["deps"]:
+            if d[1] in t.get("same", ()):
+                continue
+            name, val, clock = done[d]
+            if val > need.get(name, (0, None))[0]:
+                need[name] = (val, clock)
+        for name, (val, clock) in sorted(need.items(), key=lambda e: -len(e[1][1])):
+            if known[q].get(name, 0) < val:
+                QS[q].wait_ge(T.sem[name], val)
+                known[q][name] = val
+                for n2, v2 in clock.items():
+                    known[q][n2] = max(known[q].get(n2, 0), v2)
+        ins = t["do"](QS[q], T, x)
+        if t.get("dma"):
+            outs[0] += 16 if t.get("out") else 0
+            continue
+        for i in ins:
+            i.then_inc(T.sem[CSEM[q]], 1)
+        count[q] += len(ins)
+        done[k] = (CSEM[q], count[q], dict(known[q]))
+    for q in CSEM:
+        g.wait_ge(T.sem[CSEM[q]], count[q])
+    g.wait_ge(T.sem.lsent, x["sent"][0])
+    g.sync.wait_ge(T.sem.outs, outs[0])

@@ -8,12 +8,13 @@ TOP_P = [(0, 1024), (1024, 2048), (2048, 3072)]
 F32, BF, F16, I32, U16 = "float32", "bfloat16", "float16", "int32", "uint16"
 SB = dict(idi=(W, I32), tpi=(W, I32), xf=(W, F32), tf=(W, F32), sti=(128, I32), off=(128 * (RO + 1), U16),
           bfl=(128 * (RO + 1), F32), xg=(512 * U * (RO + 1), F32), tg=(512 * U * RO, F32), lt1=(512 * U * RO, BF),
-          lt2=(512 * U * RO, BF), prod=(512 * U * RO, F32), pre=(64 * U * RO, F32), cmb=(64 * U * RO, F32),
-          land=(256 * U * RO, F32), tr=(224 * U * RO, F32), land8=(512 * U, F32), hh=(96 * U * RO, F16),
+          lt2=(512 * U * RO, BF), prod=(512 * U * RO, F32), pre=(64 * U * RO, F32), cmb=(96 * U * RO, F32),
+          land=(256 * U * RO, F32), tr=(192 * U * RO, F32), land8=(256 * U, F32), hh=(96 * U * RO, F16),
           ubo=(64 * U * RO, F16), ubr=(64 * U * RO, F16), tt=(32 * U * RO, F32), s2=(256 * U, F32), res=(64 * U, F32),
           u8=(64 * U, F32), ycs=(32 * U, F32), pint=(8, I32), ci=(8, I32), cf=(8, F32), cc=(8, F32), rowv=(256, F32),
           rows=(512, F32), i16=(128, F16), i32x=(128, F32), i32=(128, F32), smat=(512, F16), zmat=(144, BF),
-          da=(128, BF), db=(128, BF), dm=(128, BF), gm=(32, F32), wz=(144, F32), az=(120, F32), pvs=(512 * U * 2, F32))
+          da=(128, BF), db=(128, BF), dm=(128, BF), gm=(32, F32), wz=(144, F32), az=(120, F32), pvs=(512 * U * 2, F32),
+          one=(128, BF), crf=(32, F32), crow=(32, BF))
 SCRATCH = {k: ("sbuf", [128, n], d) for k, (n, d) in SB.items()}
 for _u in range(U):
     SCRATCH["pp%d" % _u] = ("psum", [128, 512], F32)
@@ -25,11 +26,12 @@ SEMAPHORES = (["cg", "cv", "ca", "ct", "lsent", "outs", "lst"]
               + ["sm%d" % u for u in range(U)])
 CSEM = {"g": "cg", "v": "cv", "a": "ca", "t": "ct"}
 
-EST = dict(cyc=0.00104, gat=1.56, pe=0.00052, fix=0.06, afix=0.12, hop=0.1, issue=0.5, start=2.0, row=0.05,
-           byte=0.00005, first=2.0, dstart=2.0, look=0.3, stag=(9.0, 6.0, 3.0, 0.0), direct=(0, 1), split=2, fuse=1)
-OTHERS = [dict(cyc=0.00088, gat=1.2, pe=0.00045, start=1.4, row=0.03, byte=0.00004, issue=0.3),
-          dict(cyc=0.0012, gat=1.9, pe=0.0009, start=2.0, row=0.04),
-          dict(start=2.6, row=0.08, issue=0.8, hop=0.2)]
+EST = dict(cyc=0.00095, gat=1.5, pe=0.00048, fix=0.05, afix=0.1, hop=0.07, issue=0.3, start=1.4, row=0.025,
+           byte=0.00004, far=0.00008, first=1.5, dstart=1.5, look=0.3, stag=(6.0, 4.0, 2.0, 0.0), direct=(0, 1), split=2, fuse=1)
+OTHERS = [dict(cyc=0.00083, gat=1.1, pe=0.00042, start=1.5),
+          dict(cyc=0.00115, gat=1.9, pe=0.00058, start=1.2, row=0.02),
+          dict(cyc=0.0009, gat=1.8, pe=0.00045, start=1.0, row=0.02, hop=0.05, issue=0.2),
+          dict(start=1.9, row=0.04, issue=0.5)]
 TRIES, SEED = 3000, 1
 
 
@@ -51,8 +53,8 @@ def tasks_of(E):
     def pe(n, k):
         return n * E["pe"] + 0.01 * k
 
-    def rows(k, b):
-        return k * (E["row"] + b * E["byte"])
+    def rows(k, b, w="byte"):
+        return k * (E["row"] + b * E[w])
 
     def setup(s):
         prev = []
@@ -69,8 +71,9 @@ def tasks_of(E):
             add(s, "ld_" + sem, q, 0.05, [], do, lat=E["dstart"], dma=True, pin=-100 + len(prev))
             add(s, sem, "A", rows(8, nb), ["ld_" + sem] + prev[-1:], sem=(sem, 16))
             prev.append(sem)
-        add(s, "io_p", "g", 0.15, [], lambda Q, T, x: [Q.iota(T.pint[:, 0:1], [[0, 1]], 0, 1)], pin=-3)
-        add(s, "io_r", "g", 0.6, [], lambda Q, T, x: [Q.iota(T.rowv[:, :], [[1, 256]], -64, 0, allow_small_or_imprecise_dtypes=True)], pin=-2)
+        add(s, "io_p", "g", 0.15, [], lambda Q, T, x: [Q.iota(T.pint[:, 0:1], [[0, 1]], 0, 1)], pin=-4)
+        add(s, "io_r", "g", 0.6, [], lambda Q, T, x: [Q.iota(T.rowv[:, :], [[1, 256]], -64, 0, allow_small_or_imprecise_dtypes=True)], pin=-3)
+        add(s, "io_c", "g", 0.2, [], lambda Q, T, x: [Q.iota(T.crf[:, :], [[-1, 2], [0, 8], [1, 2]], 0, 0, allow_small_or_imprecise_dtypes=True)], pin=-2)
         add(s, "io_s", "g", 1.0, [], lambda Q, T, x: [Q.iota(T.rows[:, :], [[8, 4], [1, 8], [0, 16]], 0, 0, allow_small_or_imprecise_dtypes=True)], pin=-1)
         bits = [(A.arith_shift_right, 4), (A.bitwise_and, 15), (A.bitwise_and, 31), (A.bitwise_and, 7),
                 (A.arith_shift_right, 3), (A.arith_shift_right, 6), (A.bitwise_and, 112), (A.bitwise_and, 127)]
@@ -87,7 +90,6 @@ def tasks_of(E):
         col("c_nl", 0, ["cf"], ("cf", 1), 15.0, None, A.is_lt)
         col("c_s", 1, ["c_nl"], ("cc", 0), 2.0, -1.0, A.mult, A.add)
         col("c_s32", 2, ["c_nl"], ("cc", 0), 2.0 / 32, -1.0 / 32, A.mult, A.add)
-        col("c_n32", 6, ["c_nl"], ("cc", 0), -2.0 / 32, 1.0 / 32, A.mult, A.add)
         col("c_nx", 3, ["c_nl"], ("cc", 0), 16.0, ("cf", 7), A.mult, A.add)
         col("c_w", 4, ["cf"], ("cf", 3), 16.0, ("cf", 4), A.mult, A.add)
         col("c_ws", 5, ["cf"], ("cf", 5), -31.0, 32.0, A.mult, A.add)
@@ -96,9 +98,9 @@ def tasks_of(E):
             ts(name, n, deps, out, src, c, w, *([A.is_equal] if w is None else [A.is_equal, A.mult]))
         rv = lambda base, n: (lambda T: T.rowv[:, 64 + base:64 + base + n])
         mat("m_g0", 8, ["cf", "io_r"], lambda T: T.gm[:, 16:32:2], lambda T: T.rowv[:, 64:192:16], ("cf", 7), 1.0 / 32)
-        mat("m_g1", 8, ["cf", "io_r"], lambda T: T.gm[:, 17:32:2], lambda T: T.rowv[:, 64:192:16], ("cf", 7), -1.0 / 32)
+        mat("m_g1", 8, ["cf", "io_r"], lambda T: T.gm[:, 17:32:2], lambda T: T.rowv[:, 64:192:16], ("cf", 7), 1.0 / 32)
         mat("m_g", 8, ["c_s32", "io_r"], lambda T: T.gm[:, 0:16:2], rv(0, 8), ("cf", 0), ("cc", 2))
-        mat("m_gn", 8, ["c_n32", "io_r"], lambda T: T.gm[:, 1:16:2], rv(0, 8), ("cf", 0), ("cc", 6))
+        mat("m_gn", 8, ["c_s32", "io_r"], lambda T: T.gm[:, 1:16:2], rv(0, 8), ("cf", 0), ("cc", 2))
         mat("m_i16", 128, ["cf", "io_r"], lambda T: T.i16[:, :], rv(0, 128), ("cf", 7), None)
         mat("m_i1", 128, ["cf", "io_r"], lambda T: T.i32[:, :], rv(0, 128), ("cf", 7), None)
         mat("m_i32", 128, ["cf", "io_r"], lambda T: T.i32x[:, :], rv(0, 128), ("cf", 7), 32.0)
@@ -110,6 +112,8 @@ def tasks_of(E):
         mat("m_w", 144, ["c_w", "io_r"], lambda T: T.wz[:, :], rv(-12, 144), ("cc", 4), None)
         mat("m_a", 120, ["c_s", "io_r"], lambda T: T.az[:, :], rv(-56, 120), ("cf", 0), ("cc", 1))
         add(s, "ubz", "v", v(32 * U * RO), [], lambda Q, T, x: [Q.memset(T.ubo[96:128, :], 0.0)])
+        add(s, "m_one", "v", v(64), [], lambda Q, T, x: [Q.memset(T.one[0:32, :], 1.0)])
+        add(s, "m_c", "v", v(32), ["io_c"], lambda Q, T, x: [Q.tensor_scalar(T.crow[:, :], T.crf[:, :], 0.0, -x["d"], A.not_equal, A.mult)])
         for k, (lo, hi) in enumerate(IDS_P):
             ts("cvi%d" % k, hi - lo, ["li%d" % k, "c_s"], lambda T, lo=lo, hi=hi: T.xf[:, lo:hi], lambda T, lo=lo, hi=hi: T.idi[:, lo:hi], ("cc", 1), None, A.mult)
         cvp = []
@@ -123,7 +127,7 @@ def tasks_of(E):
 
     def out(s, name, deps, dst, src, stag):
         add(s, name, "s", 0.05, deps, lambda Q, T, x: [Q.dma_start(dst(T), src(T)).then_inc(T.sem.outs, 16)],
-            lat=E["dstart"] + 0.5, dma=True, out=True, stag=stag)
+            lat=E["dstart"] + 0.4, dma=True, out=True, stag=stag)
 
     def unit(s, u, loaded, cvi, cvp):
         own = (u % 2 == s)
@@ -132,10 +136,11 @@ def tasks_of(E):
         B = lambda T: T["pq%d" % u]
         offs = lambda T, r: T.off[:, 128 * r + 32 * u:128 * r + 32 * u + 32]
         bfl = lambda T, r: T.bfl[:, 128 * r + 32 * u:128 * r + 32 * u + 32]
-        l8 = lambda T, i, k=1: T.land8[:, 512 * u + 64 * i:512 * u + 64 * (i + k)]
+        l8 = lambda T, i, k=1: T.land8[:, 256 * u + 32 * i:256 * u + 32 * (i + k)]
         tt = lambda T, r: T.tt[:, 32 * (U * r + u):32 * (U * r + u) + 32]
         big = lambda T, nm, r, k=0, n=1: T[nm][:, 512 * (U * r + u) + k:512 * (U * r + u + 1):n]
         rem = dict(lat=E["start"], dma=True)
+        co = 0 if own else 16
 
         def gx(r, deps):
             add(s, "gx%d_%d" % (r, u), "a", gat, deps + cvi, lambda Q, T, x: [Q.activation(big(T, "xg", r), T.xf[:, 0:W].indirect(offs(T, r)), CP)])
@@ -144,40 +149,50 @@ def tasks_of(E):
             add(s, "gt%d_%d" % (r, u), "a", gat, deps + cvp, lambda Q, T, x: [Q.activation(big(T, "tg", r), T.tf[:, 0:W].indirect(offs(T, r)), CP)])
 
         def tform(name, nm, rr, gc, deps, ks):
-            add(s, name, "t", pe(256 * len(ks), len(ks)), deps, lambda Q, T, x: [Q.matmul(
-                B(T)[:, 160 + 16 * k:176 + 16 * k], big(T, nm, rr, k, 4), T.gm[:, gc:gc + 16], True, True) for k in ks])
+            def do(Q, T, x):
+                ins = []
+                for k in ks:
+                    o = B(T)[:, 160 + 16 * k:176 + 16 * k]
+                    ins += [Q.matmul(o, T.one[0:1, :], T.crow[0:1, co:co + 16], True, False),
+                            Q.matmul(o, big(T, nm, rr, k, 4), T.gm[:, gc:gc + 16], False, True)]
+                return ins
+            add(s, name, "t", pe(320 * len(ks), 2 * len(ks)), deps + ["m_one", "m_c"], do)
 
         def rnd(r, td):
             n = lambda w: "%s%d_%d" % (w, r, u)
             ru = U * r + u
-            ld = lambda T, i, k=1: T.land[:, 256 * ru + 64 * i:256 * ru + 64 * (i + k)]
+            ld = lambda T, i, k=1: T.land[:, 256 * ru + 32 * i:256 * ru + 32 * (i + k)]
             pre = lambda T: T.pre[:, 64 * ru:64 * ru + 64]
-            cmb = lambda T: T.cmb[:, 64 * ru:64 * ru + 64]
+            cmb = lambda T, lo, hi, st=1: T.cmb[:, 96 * ru + lo:96 * ru + hi:st]
             hh = lambda T, i, k=1: T.hh[:, 96 * ru + 32 * i:96 * ru + 32 * (i + k)]
             ubs = lambda T, nm, p: T[nm][0:p, 128 * (2 * r + u // 2):128 * (2 * r + u // 2 + 1)]
             ub = lambda T: ubs(T, "ubo" if own else "ubr", 96)
-            tr = lambda T, lo, hi, st=1: T.tr[:, 224 * ru + lo:224 * ru + hi:st]
-            mx = lambda T: tr(T, 128, 192, 2)
-            cur = lambda T: B(T)[:, 160:224]
+            tr = lambda T, i, k=1: T.tr[:, 192 * ru + 32 * i:192 * ru + 32 * (i + k)]
+            mx = lambda T: tr(T, 2)
+            cur = lambda T, o=0, st=1: B(T)[:, 160 + o:224:st]
             direct = r == 0 and u in E["direct"]
             iss = E["issue"] + (E["first"] if r == 0 and u == (0 if 0 in E["direct"] else s) else 0.0)
             if own:
-                add(s, n("Tc"), "v", v(64), td, lambda Q, T, x: [Q.tensor_scalar(l8(T, x["rank"]) if direct else pre(T), cur(T), -(END - 1) / 32.0, None, A.max)])
                 if direct:
+                    add(s, n("Tc"), "v", v(32), td, lambda Q, T, x: [Q.tensor_scalar(l8(T, x["rank"]), cur(T, 0, 2), END / 32.0 - x["d"], None, A.min)])
                     add(s, n("s1"), "g", iss, [n("Tc")], lambda Q, T, x: hop1(x, l8(T, x["rank"]), l8(T, x["rank"]), u, n("ha"), False), **rem)
-                    add(s, n("w1"), "A", rows(48, 256), [n("s1")])
+                    add(s, n("w1"), "A", rows(48, 128, "far"), [n("s1")])
                     add(s, n("ha"), None, 0, [n("w1"), (1 - s, n("w1")), (1 - s, n("w1b"))], sem=(n("ha"), "all"))
-                    add(s, n("x8"), "v", v(512), [n("ha"), n("Tc")], lambda Q, T, x: [Q.tensor_tensor(ld(T, 0, 4), l8(T, 0, 4), l8(T, 4, 4), A.max)])
+                    add(s, n("x8"), "v", v(256), [n("ha"), n("Tc")], lambda Q, T, x: [Q.tensor_tensor(ld(T, 0, 4), l8(T, 0, 4), l8(T, 4, 4), A.max)])
+                    add(s, n("y8"), "v", v(256), [n("ha"), n("Tc")], lambda Q, T, x: [Q.tensor_tensor(ld(T, 4, 4), l8(T, 0, 4), l8(T, 4, 4), A.min)])
                 else:
+                    add(s, n("Tc"), "v", v(64), td, lambda Q, T, x: [Q.tensor_scalar(pre(T), cur(T), END / 32.0 - x["d"], None, A.min)])
                     add(s, n("s0"), "g", iss, [n("Tc")], lambda Q, T, x: tosib(x, pre(T), n("hp")), **rem)
                     add(s, n("w0"), "B", rows(16, 256), [n("s0")] + loaded)
                     add(s, n("ha"), None, 0, [(1 - s, n("w1")), (1 - s, n("w1b"))], sem=(n("ha"), None))
-                add(s, n("xa"), "v", v(256), [n("x8" if direct else "ha")], lambda Q, T, x: [Q.tensor_tensor(tr(T, 0, 128), ld(T, 0, 2), ld(T, 2, 2), A.max)])
-                add(s, n("xb"), "v", v(128), [n("xa")], lambda Q, T, x: [Q.tensor_tensor(tr(T, 128, 192), tr(T, 0, 64), tr(T, 64, 128), A.max)])
+                yo = 4 if direct else 0
+                add(s, n("xa"), "v", v(128), [n("x8" if direct else "ha")], lambda Q, T, x: [Q.tensor_tensor(tr(T, 0, 2), ld(T, 0, 2), ld(T, 2, 2), A.max)])
+                add(s, n("ya"), "v", v(128), [n("y8" if direct else "ha")], lambda Q, T, x: [Q.tensor_tensor(tr(T, 3, 2), ld(T, yo, 2), ld(T, yo + 2, 2), A.min)])
+                add(s, n("xb"), "v", v(64), [n("xa")], lambda Q, T, x: [Q.tensor_tensor(tr(T, 2), tr(T, 0), tr(T, 1), A.max)])
+                add(s, n("yb"), "v", v(64), [n("ya")], lambda Q, T, x: [Q.tensor_tensor(tr(T, 5), tr(T, 3), tr(T, 4), A.min)])
                 add(s, n("hi"), "v", v(32), [n("xb")], lambda Q, T, x: [Q.tensor_copy(hh(T, 0), mx(T))])
-                add(s, n("df"), "v", v(64), [n("xb")], lambda Q, T, x: [Q.tensor_tensor(tr(T, 192, 224), mx(T), tr(T, 129, 192, 2), A.add)])
                 add(s, n("lo"), "v", v(64), [n("hi")], lambda Q, T, x: [Q.tensor_tensor(hh(T, 1), mx(T), hh(T, 0), A.subtract)])
-                add(s, n("ht"), "v", v(32), [n("df")], lambda Q, T, x: [Q.tensor_scalar(hh(T, 2), tr(T, 192, 224), 0.0, None, A.is_le)])
+                add(s, n("ht"), "v", v(64), [n("xb"), n("yb")], lambda Q, T, x: [Q.tensor_tensor(hh(T, 2), tr(T, 5), mx(T), A.is_ge)])
                 add(s, n("tt"), "v", v(64), [n("ht")], lambda Q, T, x: [Q.tensor_tensor(tt(T, r), mx(T), hh(T, 2), A.mult)])
                 if r:
                     add(s, n("ts"), "v", v(64), [n("tt"), ("ts%d_%d" if r > 1 else "tt%d_%d") % (r - 1, u)], lambda Q, T, x: [Q.tensor_tensor(tt(T, r), tt(T, r), tt(T, r - 1), A.add)])
@@ -188,14 +203,15 @@ def tasks_of(E):
                 hd = [n("Uc")]
             else:
                 if direct:
-                    add(s, n("Tc"), "v", v(64), td, lambda Q, T, x: [Q.tensor_copy(l8(T, x["rank"]), cur(T))])
+                    add(s, n("Tc"), "v", v(32), td, lambda Q, T, x: [Q.tensor_copy(l8(T, x["rank"]), cur(T, 1, 2))])
                     add(s, n("s1"), "g", iss, [n("Tc")], lambda Q, T, x: hop1(x, l8(T, x["rank"]), l8(T, x["rank"]), u, n("ha"), True), **rem)
                 else:
                     add(s, n("hp"), None, 0, [(1 - s, n("w0"))], sem=(n("hp"), None))
-                    add(s, n("Tc"), "v", v(64), td + [n("hp")], lambda Q, T, x: [Q.tensor_tensor(cmb(T), pre(T), cur(T), A.max)])
-                    add(s, n("s1"), "g", E["issue"], [n("Tc")], lambda Q, T, x: hop1(x, cmb(T), ld(T, x["slot"]), u, n("ha"), True), **rem)
-                add(s, n("w1"), "A", rows(48, 256), [n("s1")])
-                add(s, n("w1b"), "B", rows(16, 256), [n("s1")] + loaded)
+                    add(s, n("Tc"), "v", v(64), td + [n("hp")], lambda Q, T, x: [Q.tensor_tensor(cmb(T, 0, 64), pre(T), cur(T), A.max)])
+                    add(s, n("Td"), "v", v(64), [n("Tc")], lambda Q, T, x: [Q.tensor_tensor(cmb(T, 64, 96), cmb(T, 0, 64, 2), cmb(T, 1, 64, 2), A.min)])
+                    add(s, n("s1"), "g", E["issue"], [n("Td")], lambda Q, T, x: hop1(x, cmb(T, 64, 96), ld(T, x["slot"]), u, n("ha"), True), **rem)
+                add(s, n("w1"), "A", rows(48, 128, "far"), [n("s1")])
+                add(s, n("w1b"), "B", rows(16, 128), [n("s1")] + loaded)
                 add(s, n("hb"), None, 0, [(1 - s, n("w2"))], sem=(n("hb"), None))
                 hd = [n("hb"), n("Tc")]
             add(s, n("B"), "t", pe(512, 4), hd + ["m_s"], lambda Q, T, x: [Q.matmul(
@@ -411,8 +427,9 @@ def rank_program(g, core, T, topo):
             moff &= topo.mask(core, c)
     mon = topo.mask(core, sib) & ~moff
     noff, non = bin(moff).count("1"), bin(mon).count("1")
+    slot = pairs.index(mine)
     x = dict(g=g, T=T, topo=topo, pairs=pairs, sib=sib, moff=moff, mon=mon, noff=noff, non=non, sent=[0],
-             rank=rank, slot=pairs.index(mine))
+             rank=rank, slot=slot, d=(0.25 if slot == 0 else 0.5) / 32)
     QS = {"g": g, "v": g.vector, "a": g.scalar, "t": g.tensor, "s": g.sync}
     count = {q: 0 for q in CSEM}
     known = {q: {} for q in QS}

import numpy as np
from concourse.bass import DstId, RemoteDMATransfer
from concourse.mybir import AluOpType, ActivationFunctionType

W, END, RO, U = 3072, 2 ** 20 - 1, 3, 4
IDS_P = [(0, 1024), (1024, 2048), (2048, 2816), (2816, 3072)]
TOP_P = [(0, 1024), (1024, 2048), (2048, 3072)]
F32, BF, F16, I32, U16 = "float32", "bfloat16", "float16", "int32", "uint16"
SB = dict(idi=(W, I32), tpi=(W, I32), xf=(W, F32), tf=(W, F32), sti=(128, I32), off=(128 * (RO + 1), U16),
          bfl=(128 * (RO + 1), F32), xg=(512 * U * (RO + 1), F32), tg=(512 * U * RO, F32), lt1=(512 * U * RO, BF),
          lt2=(512 * U * RO, BF), prod=(512 * U * RO, F32), pre=(64 * U * RO, F32), cmb=(96 * U * RO, F32),
          land=(256 * U * RO, F32), tr=(192 * U * RO, F32), land8=(256 * U, F32), hh=(96 * U * RO, F16),
          ubo=(64 * U * RO, F16), ubr=(64 * U * RO, F16), tt=(32 * U * RO, F32), s2=(256 * U, F32), res=(64 * U, F32),
          u8=(64 * U, F32), ycs=(32 * U, F32), pint=(8, I32), ci=(8, I32), cf=(8, F32), cc=(8, F32), rowv=(256, F32),
          rows=(512, F32), i16=(128, F16), i32x=(128, F32), i32=(128, F32), smat=(512, F16), zmat=(144, BF),
          da=(128, BF), db=(128, BF), dm=(128, BF), gm=(32, F32), wz=(144, F32), az=(120, F32), pvs=(512 * U * 2, F32),
          one=(128, BF), crf=(32, F32), crow=(32, BF))
SCRATCH = {k: ("sbuf", [128, n], d) for k, (n, d) in SB.items()}
for _u in range(U):
    SCRATCH["pp%d" % _u] = ("psum", [128, 512], F32)
    SCRATCH["pq%d" % _u] = ("psum", [128, 512], F32)

SEMAPHORES = (["cg", "cv", "ca", "ct", "lsent", "outs", "lst"]
              + ["li%d" % i for i in range(len(IDS_P))] + ["lp%d" % i for i in range(len(TOP_P))]
              + ["%s%d_%d" % (w, r, u) for w in ("hp", "ha", "hb") for r in range(RO) for u in range(U)]
              + ["sm%d" % u for u in range(U)])
CSEM = {"g": "cg", "v": "cv", "a": "ca", "t": "ct"}

EST = dict(cyc=0.00095, gat=1.5, pe=0.00048, fix=0.05, afix=0.1, hop=0.07, issue=0.3, start=1.4, row=0.025,
           byte=0.00004, far=0.00008, first=1.5, dstart=1.5, look=0.3, stag=(6.0, 4.0, 2.0, 0.0), direct=(0, 1), split=2, fuse=1)
OTHERS = [dict(cyc=0.00083, gat=1.1, pe=0.00042, start=1.5),
          dict(cyc=0.00115, gat=1.9, pe=0.00058, start=1.2, row=0.02),
          dict(cyc=0.0009, gat=1.8, pe=0.00045, start=1.0, row=0.02, hop=0.05, issue=0.2),
          dict(start=1.9, row=0.04, issue=0.5)]
TRIES, SEED = 3000, 1


def tasks_of(E):
    K = {}
    A = AluOpType
    CP = ActivationFunctionType.Copy
    S = E["split"]

    def add(s, name, q, dur, deps, do=None, lat=0.0, sem=None, **kw):
        K[(s, name)] = dict(q=q, dur=dur, deps=[d if isinstance(d, tuple) else (s, d) for d in deps], do=do, lat=lat, sem=sem, **kw)

    def v(n):
        return E["fix"] + max(64, n) * E["cyc"]

    def a(n):
        return E["afix"] + n * E["cyc"]

    def pe(n, k):
        return n * E["pe"] + 0.01 * k

    def rows(k, b, w="byte"):
        return k * (E["row"] + b * E[w])

    def setup(s):
        prev = []
        order = [("i", 0), ("st", 0), ("i", 1), ("i", 2), ("i", 3)] + [("p", k) for k in range(len(TOP_P))]
        for kind, k in order:
            if kind == "st":
                q, sem, nb = "a", "lst", 512
                do = lambda Q, T, x: [Q.dma_start(T.sti[:, :], T.st[:, :]).then_inc(T.sem.lst, 16)]
            else:
                lo, hi = (IDS_P if kind == "i" else TOP_P)[k]
                q, sem, nb = ("a" if (kind, k) == ("i", 1) else "s"), "l%s%d" % (kind, k), 4 * (hi - lo)
                do = lambda Q, T, x, kind=kind, lo=lo, hi=hi, sem=sem: [Q.dma_start(
                    T["idi" if kind == "i" else "tpi"][:, lo:hi], T["ids" if kind == "i" else "tops"][:, lo:hi]).then_inc(T.sem[sem], 16)]
            add(s, "ld_" + sem, q, 0.05, [], do, lat=E["dstart"], dma=True, pin=-100 + len(prev))
            add(s, sem, "A", rows(8, nb), ["ld_" + sem] + prev[-1:], sem=(sem, 16))
            prev.append(sem)
        add(s, "io_p", "g", 0.15, [], lambda Q, T, x: [Q.iota(T.pint[:, 0:1], [[0, 1]], 0, 1)], pin=-4)
        add(s, "io_r", "g", 0.6, [], lambda Q, T, x: [Q.iota(T.rowv[:, :], [[1, 256]], -64, 0, allow_small_or_imprecise_dtypes=True)], pin=-3)
        add(s, "io_c", "g", 0.2, [], lambda Q, T, x: [Q.iota(T.crf[:, :], [[-1, 2], [0, 8], [1, 2]], 0, 0, allow_small_or_imprecise_dtypes=True)], pin=-2)
        add(s, "io_s", "g", 1.0, [], lambda Q, T, x: [Q.iota(T.rows[:, :], [[8, 4], [1, 8], [0, 16]], 0, 0, allow_small_or_imprecise_dtypes=True)], pin=-1)
        bits = [(A.arith_shift_right, 4), (A.bitwise_and, 15), (A.bitwise_and, 31), (A.bitwise_and, 7),
                (A.arith_shift_right, 3), (A.arith_shift_right, 6), (A.bitwise_and, 112), (A.bitwise_and, 127)]
        for j, (op, n) in enumerate(bits):
            add(s, "ci%d" % j, "v", v(1), ["io_p"], lambda Q, T, x, j=j, op=op, n=n: [Q.tensor_scalar(T.ci[:, j:j + 1], T.pint[:, 0:1], n, None, op)])
        add(s, "cf", "v", v(8), ["ci%d" % j for j in range(8)], lambda Q, T, x: [Q.tensor_copy(T.cf[:, :], T.ci[:, :])])
        cl = lambda T, c: (T[c[0]][:, c[1]:c[1] + 1] if isinstance(c, tuple) else c)

        def ts(name, n, deps, out, src, s1, s2, *ops):
            add(s, name, "v", v(n), deps, lambda Q, T, x: [Q.tensor_scalar(out(T), src(T), cl(T, s1), cl(T, s2), *ops)])

        def col(name, j, deps, src, *rest):
            ts(name, 1, deps, lambda T: T.cc[:, j:j + 1], lambda T: cl(T, src), *rest)
        col("c_nl", 0, ["cf"], ("cf", 1), 15.0, None, A.is_lt)
        col("c_s", 1, ["c_nl"], ("cc", 0), 2.0, -1.0, A.mult, A.add)
        col("c_s32", 2, ["c_nl"], ("cc", 0), 2.0 / 32, -1.0 / 32, A.mult, A.add)
        col("c_nx", 3, ["c_nl"], ("cc", 0), 16.0, ("cf", 7), A.mult, A.add)
        col("c_w", 4, ["cf"], ("cf", 3), 16.0, ("cf", 4), A.mult, A.add)
        col("c_ws", 5, ["cf"], ("cf", 5), -31.0, 32.0, A.mult, A.add)

        def mat(name, n, deps, out, src, c, w):
            ts(name, n, deps, out, src, c, w, *([A.is_equal] if w is None else [A.is_equal, A.mult]))
        rv = lambda base, n: (lambda T: T.rowv[:, 64 + base:64 + base + n])
        mat("m_g0", 8, ["cf", "io_r"], lambda T: T.gm[:, 16:32:2], lambda T: T.rowv[:, 64:192:16], ("cf", 7), 1.0 / 32)
        mat("m_g1", 8, ["cf", "io_r"], lambda T: T.gm[:, 17:32:2], lambda T: T.rowv[:, 64:192:16], ("cf", 7), 1.0 / 32)
        mat("m_g", 8, ["c_s32", "io_r"], lambda T: T.gm[:, 0:16:2], rv(0, 8), ("cf", 0), ("cc", 2))
        mat("m_gn", 8, ["c_s32", "io_r"], lambda T: T.gm[:, 1:16:2], rv(0, 8), ("cf", 0), ("cc", 2))
        mat("m_i16", 128, ["cf", "io_r"], lambda T: T.i16[:, :], rv(0, 128), ("cf", 7), None)
        mat("m_i1", 128, ["cf", "io_r"], lambda T: T.i32[:, :], rv(0, 128), ("cf", 7), None)
        mat("m_i32", 128, ["cf", "io_r"], lambda T: T.i32x[:, :], rv(0, 128), ("cf", 7), 32.0)
        mat("m_s", 512, ["c_ws", "io_s"], lambda T: T.smat[:, :], lambda T: T.rows[:, :], ("cf", 2), ("cc", 5))
        mat("m_z", 144, ["cf", "io_r"], lambda T: T.zmat[:, :], rv(-15, 144), ("cf", 6), None)
        mat("m_da", 128, ["c_nx", "io_r"], lambda T: T.da[:, :], rv(15, 128), ("cc", 3), None)
        mat("m_db", 128, ["c_nl", "io_r"], lambda T: T.db[:, :], rv(0, 128), ("cf", 7), ("cc", 0))
        add(s, "m_d", "v", v(256), ["m_da", "m_db"], lambda Q, T, x: [Q.tensor_tensor(T.dm[:, :], T.da[:, :], T.db[:, :], A.subtract)])
        mat("m_w", 144, ["c_w", "io_r"], lambda T: T.wz[:, :], rv(-12, 144), ("cc", 4), None)
        mat("m_a", 120, ["c_s", "io_r"], lambda T: T.az[:, :], rv(-56, 120), ("cf", 0), ("cc", 1))
        add(s, "ubz", "v", v(32 * U * RO), [], lambda Q, T, x: [Q.memset(T.ubo[96:128, :], 0.0)])
        add(s, "m_one", "v", v(64), [], lambda Q, T, x: [Q.memset(T.one[0:32, :], 1.0)])
        add(s, "m_c", "v", v(32), ["io_c"], lambda Q, T, x: [Q.tensor_scalar(T.crow[:, :], T.crf[:, :], 0.0, -x["d"], A.not_equal, A.mult)])
        for k, (lo, hi) in enumerate(IDS_P):
            ts("cvi%d" % k, hi - lo, ["li%d" % k, "c_s"], lambda T, lo=lo, hi=hi: T.xf[:, lo:hi], lambda T, lo=lo, hi=hi: T.idi[:, lo:hi], ("cc", 1), None, A.mult)
        cvp = []
        for k, (lo, hi) in enumerate(TOP_P):
            for l2 in range(lo, hi, 512):
                cvp.append("cvp%d" % l2)
                add(s, cvp[-1], "v", v(512), ["lp%d" % k], lambda Q, T, x, l2=l2: [Q.tensor_copy(T.tf[:, l2:l2 + 512], T.tpi[:, l2:l2 + 512])])
        add(s, "off0", "v", v(128), ["lst"], lambda Q, T, x: [Q.tensor_copy(T.off[:, 0:128], T.sti[:, :])])
        add(s, "bfl0", "v", v(128), ["lst"], lambda Q, T, x: [Q.tensor_copy(T.bfl[:, 0:128], T.sti[:, :])])
        return prev[-1:], ["cvi%d" % k for k in range(len(IDS_P))], cvp

    def out(s, name, deps, dst, src, stag):
        add(s, name, "s", 0.05, deps, lambda Q, T, x: [Q.dma_start(dst(T), src(T)).then_inc(T.sem.outs, 16)],
            lat=E["dstart"] + 0.4, dma=True, out=True, stag=stag)

    def unit(s, u, loaded, cvi, cvp):
        own = (u % 2 == s)
        gat = E["afix"] + 512 * E["cyc"] * E["gat"]
        P = lambda T: T["pp%d" % u]
        B = lambda T: T["pq%d" % u]
        offs = lambda T, r: T.off[:, 128 * r + 32 * u:128 * r + 32 * u + 32]
        bfl = lambda T, r: T.bfl[:, 128 * r + 32 * u:128 * r + 32 * u + 32]
        l8 = lambda T, i, k=1: T.land8[:, 256 * u + 32 * i:256 * u + 32 * (i + k)]
        tt = lambda T, r: T.tt[:, 32 * (U * r + u):32 * (U * r + u) + 32]
        big = lambda T, nm, r, k=0, n=1: T[nm][:, 512 * (U * r + u) + k:512 * (U * r + u + 1):n]
        rem = dict(lat=E["start"], dma=True)
        co = 0 if own else 16

        def gx(r, deps):
            add(s, "gx%d_%d" % (r, u), "a", gat, deps + cvi, lambda Q, T, x: [Q.activation(big(T, "xg", r), T.xf[:, 0:W].indirect(offs(T, r)), CP)])

        def gt(r, deps):
            add(s, "gt%d_%d" % (r, u), "a", gat, deps + cvp, lambda Q, T, x: [Q.activation(big(T, "tg", r), T.tf[:, 0:W].indirect(offs(T, r)), CP)])

        def tform(name, nm, rr, gc, deps, ks):
            def do(Q, T, x):
                ins = []
                for k in ks:
                    o = B(T)[:, 160 + 16 * k:176 + 16 * k]
                    ins += [Q.matmul(o, T.one[0:1, :], T.crow[0:1, co:co + 16], True, False),
                            Q.matmul(o, big(T, nm, rr, k, 4), T.gm[:, gc:gc + 16], False, True)]
                return ins
            add(s, name, "t", pe(320 * len(ks), 2 * len(ks)), deps + ["m_one", "m_c"], do)

        def rnd(r, td):
            n = lambda w: "%s%d_%d" % (w, r, u)
            ru = U * r + u
            ld = lambda T, i, k=1: T.land[:, 256 * ru + 32 * i:256 * ru + 32 * (i + k)]
            pre = lambda T: T.pre[:, 64 * ru:64 * ru + 64]
            cmb = lambda T, lo, hi, st=1: T.cmb[:, 96 * ru + lo:96 * ru + hi:st]
            hh = lambda T, i, k=1: T.hh[:, 96 * ru + 32 * i:96 * ru + 32 * (i + k)]
            ubs = lambda T, nm, p: T[nm][0:p, 128 * (2 * r + u // 2):128 * (2 * r + u // 2 + 1)]
            ub = lambda T: ubs(T, "ubo" if own else "ubr", 96)
            tr = lambda T, i, k=1: T.tr[:, 192 * ru + 32 * i:192 * ru + 32 * (i + k)]
            mx = lambda T: tr(T, 2)
            cur = lambda T, o=0, st=1: B(T)[:, 160 + o:224:st]
            direct = r == 0 and u in E["direct"]
            iss = E["issue"] + (E["first"] if r == 0 and u == (0 if 0 in E["direct"] else s) else 0.0)
            if own:
                if direct:
                    add(s, n("Tc"), "v", v(32), td, lambda Q, T, x: [Q.tensor_scalar(l8(T, x["rank"]), cur(T, 0, 2), END / 32.0 - x["d"], None, A.min)])
                    add(s, n("s1"), "g", iss, [n("Tc")], lambda Q, T, x: hop1(x, l8(T, x["rank"]), l8(T, x["rank"]), u, n("ha"), False), **rem)
                    add(s, n("w1"), "A", rows(48, 128, "far"), [n("s1")])
                    add(s, n("ha"), None, 0, [n("w1"), (1 - s, n("w1")), (1 - s, n("w1b"))], sem=(n("ha"), "all"))
                    add(s, n("x8"), "v", v(256), [n("ha"), n("Tc")], lambda Q, T, x: [Q.tensor_tensor(ld(T, 0, 4), l8(T, 0, 4), l8(T, 4, 4), A.max)])
                    add(s, n("y8"), "v", v(256), [n("ha"), n("Tc")], lambda Q, T, x: [Q.tensor_tensor(ld(T, 4, 4), l8(T, 0, 4), l8(T, 4, 4), A.min)])
                else:
                    add(s, n("Tc"), "v", v(64), td, lambda Q, T, x: [Q.tensor_scalar(pre(T), cur(T), END / 32.0 - x["d"], None, A.min)])
                    add(s, n("s0"), "g", iss, [n("Tc")], lambda Q, T, x: tosib(x, pre(T), n("hp")), **rem)
                    add(s, n("w0"), "B", rows(16, 256), [n("s0")] + loaded)
                    add(s, n("ha"), None, 0, [(1 - s, n("w1")), (1 - s, n("w1b"))], sem=(n("ha"), None))
                yo = 4 if direct else 0
                add(s, n("xa"), "v", v(128), [n("x8" if direct else "ha")], lambda Q, T, x: [Q.tensor_tensor(tr(T, 0, 2), ld(T, 0, 2), ld(T, 2, 2), A.max)])
                add(s, n("ya"), "v", v(128), [n("y8" if direct else "ha")], lambda Q, T, x: [Q.tensor_tensor(tr(T, 3, 2), ld(T, yo, 2), ld(T, yo + 2, 2), A.min)])
                add(s, n("xb"), "v", v(64), [n("xa")], lambda Q, T, x: [Q.tensor_tensor(tr(T, 2), tr(T, 0), tr(T, 1), A.max)])
                add(s, n("yb"), "v", v(64), [n("ya")], lambda Q, T, x: [Q.tensor_tensor(tr(T, 5), tr(T, 3), tr(T, 4), A.min)])
                add(s, n("hi"), "v", v(32), [n("xb")], lambda Q, T, x: [Q.tensor_copy(hh(T, 0), mx(T))])
                add(s, n("lo"), "v", v(64), [n("hi")], lambda Q, T, x: [Q.tensor_tensor(hh(T, 1), mx(T), hh(T, 0), A.subtract)])
                add(s, n("ht"), "v", v(64), [n("xb"), n("yb")], lambda Q, T, x: [Q.tensor_tensor(hh(T, 2), tr(T, 5), mx(T), A.is_ge)])
                add(s, n("tt"), "v", v(64), [n("ht")], lambda Q, T, x: [Q.tensor_tensor(tt(T, r), mx(T), hh(T, 2), A.mult)])
                if r:
                    add(s, n("ts"), "v", v(64), [n("tt"), ("ts%d_%d" if r > 1 else "tt%d_%d") % (r - 1, u)], lambda Q, T, x: [Q.tensor_tensor(tt(T, r), tt(T, r), tt(T, r - 1), A.add)])
                add(s, n("U"), "t", pe(128, 1), [n("lo"), n("ht"), n("Tc"), "m_i16"], lambda Q, T, x: [Q.matmul(B(T)[0:96, 0:128], hh(T, 0, 3), T.i16[:, :], True, True)])
                add(s, n("Uc"), "v", v(128), [n("U")], lambda Q, T, x: [Q.tensor_copy(ub(T), B(T)[0:96, 0:128])])
                add(s, n("s2"), "g", E["issue"], [n("Uc"), "ubz"], lambda Q, T, x: tosib(x, ubs(T, "ubo", 128), n("hb"), ubs(T, "ubr", 128)), **rem)
                add(s, n("w2"), "B", rows(16, 256), [n("s2")])
                hd = [n("Uc")]
            else:
                if direct:
                    add(s, n("Tc"), "v", v(32), td, lambda Q, T, x: [Q.tensor_copy(l8(T, x["rank"]), cur(T, 1, 2))])
                    add(s, n("s1"), "g", iss, [n("Tc")], lambda Q, T, x: hop1(x, l8(T, x["rank"]), l8(T, x["rank"]), u, n("ha"), True), **rem)
                else:
                    add(s, n("hp"), None, 0, [(1 - s, n("w0"))], sem=(n("hp"), None))
                    add(s, n("Tc"), "v", v(64), td + [n("hp")], lambda Q, T, x: [Q.tensor_tensor(cmb(T, 0, 64), pre(T), cur(T), A.max)])
                    add(s, n("Td"), "v", v(64), [n("Tc")], lambda Q, T, x: [Q.tensor_tensor(cmb(T, 64, 96), cmb(T, 0, 64, 2), cmb(T, 1, 64, 2), A.min)])
                    add(s, n("s1"), "g", E["issue"], [n("Td")], lambda Q, T, x: hop1(x, cmb(T, 64, 96), ld(T, x["slot"]), u, n("ha"), True), **rem)
                add(s, n("w1"), "A", rows(48, 128, "far"), [n("s1")])
                add(s, n("w1b"), "B", rows(16, 128), [n("s1")] + loaded)
                add(s, n("hb"), None, 0, [(1 - s, n("w2"))], sem=(n("hb"), None))
                hd = [n("hb"), n("Tc")]
            add(s, n("B"), "t", pe(512, 4), hd + ["m_s"], lambda Q, T, x: [Q.matmul(
                P(T)[:, k:512:4], T.smat[0:96, 128 * k:128 * k + 128], ub(T), True, True) for k in range(4)])
            add(s, n("Nb"), "t", pe(256, 1), [n("B"), "m_i1", ("ba%d_%d" % (r - 1, u) if r else "bfl0")],
                lambda Q, T, x: [Q.matmul(B(T)[:, 128:160], T.i32[:, :], bfl(T, r), True, False)], same=[n("B")])
            last = n("Nb")
            for h in range(S):
                add(s, n("c1" + "ab"[h]), "v", v(512 // S), [n("B"), n("gt")], lambda Q, T, x, h=h: [Q.tensor_tensor(big(T, "lt1", r, h, S), big(T, "tg", r, h, S), P(T)[:, h:512:S], A.is_lt)])
                add(s, n("N" + "xy"[h]), "t", pe(1024 // S, 16 // S), [n("c1" + "ab"[h]), last, "m_z"], lambda Q, T, x, h=h: [Q.matmul(
                    B(T)[:, 128:160], T.zmat[:, 15 - k:143 - k], big(T, "lt1", r, k, 16), False, k == 15) for k in range(h, 16, S)], same=[last])
                last = n("N" + "xy"[h])
            add(s, n("bo"), "v", v(32), [last], lambda Q, T, x: [Q.tensor_copy(offs(T, r + 1), B(T)[:, 128:160])])
            gx(r + 1, [n("bo")])
            add(s, n("ba"), "a", a(32), [n("bo")], lambda Q, T, x: [Q.activation(bfl(T, r + 1), B(T)[:, 128:160], CP)])
            if r + 1 < RO:
                gt(r + 1, [n("bo")])
            if E["fuse"]:
                add(s, n("pc"), "a", a(512), [n("c1" + "ab"[h]) for h in range(S)], lambda Q, T, x: [Q.activation(big(T, "pvs", r % 2), P(T)[:, :], CP)])
                add(s, n("c2"), "v", E["fix"] + 512 * E["cyc"] * E["gat"], [n("bo"), n("pc")], lambda Q, T, x: [Q.tensor_tensor(big(T, "lt2", r), T.xf[:, 0:W].indirect(offs(T, r + 1)), big(T, "pvs", r % 2), A.is_lt)])
            else:
                add(s, n("c2"), "v", v(512), ["gx%d_%d" % (r + 1, u), n("B")], lambda Q, T, x: [Q.tensor_tensor(big(T, "lt2", r), big(T, "xg", r + 1), P(T)[:, :], A.is_lt)])
            add(s, n("S"), "t", pe(512, 1), [n("c2"), "m_d"], lambda Q, T, x: [Q.matmul(P(T)[:, :], T.dm[:, :], big(T, "lt2", r), True, True)])
            td = []
            for h in range(S):
                add(s, n("mu" + "ab"[h]), "v", v(512 // S), [n("S"), "gx%d_%d" % (r + 1, u)], lambda Q, T, x, h=h: [Q.tensor_tensor(big(T, "prod", r, h, S), big(T, "xg", r + 1, h, S), P(T)[:, h:512:S], A.mult)])
                if r + 1 < RO:
                    td.append(n("T" + "ab"[h]))
                    tform(td[-1], "prod", r, 0, [n("mu" + "ab"[h]), n("ba"), "m_g", "m_gn"], list(range(h, 4, S)))
            return td

        gx(0, ["off0"])
        gt(0, ["off0"])
        td = ["T_%d" % u]
        tform(td[0], "xg", 0, 16, ["gx0_%d" % u, "m_g0", "m_g1"], [0, 1, 2, 3])
        for r in range(RO):
            td = rnd(r, td)
        n = lambda w: "%s%d_%d" % (w, RO - 1, u)
        rs = lambda T, i, k=1: T.res[:, 64 * u + 32 * i:64 * u + 32 * (i + k)]
        free = [n("ba")]
        if own:
            add(s, n("HA"), "t", pe(896, 4), [n("ba"), n("ts"), "m_i32", "m_i16"], lambda Q, T, x: [
                Q.matmul(B(T)[0:32, 256:384], tt(T, RO - 1), T.i32x[:, :], True, True)] + [
                Q.matmul(B(T)[0:32, 384:512], T.hh[:, 96 * (U * r + u) + 64:96 * (U * r + u) + 96], T.i16[:, :], r == 0, r == RO - 1) for r in range(RO)])
            add(s, n("Hc"), "a", a(256), [n("HA")], lambda Q, T, x: [Q.activation(T.s2[0:32, 256 * u:256 * u + 256], B(T)[0:32, 256:512], CP)])
            add(s, n("HB"), "t", pe(1024, 4), [n("Hc"), "m_w"], lambda Q, T, x: [Q.matmul(
                B(T)[:, 192:256], T.wz[0:32, 12 - 4 * k:140 - 4 * k], T.s2[0:32, 256 * u + k:256 * u + 256:4], k == 0, k == 3) for k in range(4)])
            add(s, n("Hd"), "a", a(64), [n("HB")], lambda Q, T, x: [Q.activation(rs(T, 0, 2), B(T)[:, 192:256], CP)])
            add(s, n("s3"), "g", E["issue"], [n("Hd")], lambda Q, T, x: tosib(x, rs(T, 0, 2), "sm%d" % u), **rem)
            add(s, n("w3"), "B", rows(16, 256), [n("s3")])
            d = free = [n("Hd")]
        else:
            add(s, "sm%d" % u, None, 0, [(1 - s, n("w3"))], sem=("sm%d" % u, None))
            d = ["sm%d" % u]
        out(s, n("os"), d, lambda T: T.ys[:, 32 * u:32 * u + 32], lambda T: rs(T, 0), E["stag"][u])
        out(s, n("oh"), d, lambda T: T.yh[:, 32 * u:32 * u + 32], lambda T: rs(T, 1), E["stag"][u])
        last = []
        for h in range(S):
            add(s, n("FA" + "ab"[h]), "t", pe(2048 // S, 8 // S), [n("mu" + "ab"[h]), "m_a"] + free + last, lambda Q, T, x, h=h: [Q.matmul(
                B(T)[0:64, 0:64], T.az[:, 56 - 8 * k:120 - 8 * k], big(T, "prod", RO - 1, k, 8), k == 0, k == 7) for k in range(h, 8, S)], same=last)
            last = [n("FA" + "ab"[h])]
        add(s, n("Fc"), "a", a(64), last, lambda Q, T, x: [Q.activation(T.u8[0:64, 64 * u:64 * u + 64], B(T)[0:64, 0:64], CP)])
        add(s, n("FB"), "t", pe(512, 2), [n("Fc"), "m_w"], lambda Q, T, x: [Q.matmul(
            B(T)[:, 64:96], T.wz[0:64, 12 - 8 * k:140 - 8 * k], T.u8[0:64, 64 * u + k:64 * u + 64:2], k == 0, k == 1) for k in range(2)])
        add(s, n("Fd"), "a", a(32), [n("FB")], lambda Q, T, x: [Q.activation(T.ycs[:, 32 * u:32 * u + 32], B(T)[:, 64:96], CP)])
        out(s, n("oc"), [n("Fd")], lambda T: T.yc[:, 32 * u:32 * u + 32], lambda T: T.ycs[:, 32 * u:32 * u + 32], E["stag"][u])

    for s in (0, 1):
        pr = setup(s)
        for u in range(U):
            unit(s, u, *pr)
        out(s, "ob", ["ba%d_%d" % (RO - 1, u) for u in range(U)], lambda T: T.yb[:, :], lambda T: T.bfl[:, 128 * RO:128 * RO + 128], 0.0)
    for t in K.values():
        t["gap"] = t["lat"] + (E["hop"] if t["do"] and not t.get("dma") or t["sem"] else 0.0)
    return K


def dst_id(topo, c):
    ad = topo.addr(c)
    return DstId(rid=ad[0], pnc=ad[1])


def hop1(x, src, dst, u, sem, sib):
    T, topo = x["T"], x["topo"]
    n = len(x["pairs"])
    far = [x["pairs"][(x["slot"] + k) % n][u % 2] for k in range(1, n)]
    trs = [RemoteDMATransfer(dst_ids=[dst_id(topo, d) for d in far], dma_engine_mask=x["moff"], remote_sem=T.sem[sem],
                             srcs=[src], dsts=[dst for d in far])]
    x["sent"][0] += x["noff"]
    if sib:
        trs.append(RemoteDMATransfer(dst_ids=[dst_id(topo, x["sib"])], dma_engine_mask=x["mon"], remote_sem=T.sem[sem],
                                     srcs=[src], dsts=[dst]))
        x["sent"][0] += x["non"]
    return [x["g"].remote_dma_fused(trs, local_sem=T.sem.lsent)]


def tosib(x, src, sem, dst=None):
    ad = x["topo"].addr(x["sib"])
    x["sent"][0] += x["non"]
    return [x["g"].remote_dma(src if dst is None else dst, src, x["T"].sem[sem], x["T"].sem.lsent, ad[1], ad[0], x["mon"])]


def plan(K, E, prio):
    kids = {k: [] for k in K}
    for k, t in K.items():
        for d in t["deps"]:
            kids[d].append(k)
    tail = {}

    def way(k):
        if k not in tail:
            tail[k] = K[k]["dur"] + K[k]["gap"] + max([way(c) for c in kids[k]] + [K[k].get("stag", 0.0)])
        return tail[k]
    key = {k: (K[k].get("pin", 0), -way(k) - prio.get(k, 0.0)) for k in K}
    left = {k: len(K[k]["deps"]) for k in K}
    ready = {}
    for k in K:
        if left[k] == 0:
            ready.setdefault((k[0], K[k]["q"]), []).append(k)
    rt = {k: 0.0 for k in K}
    free, order, end = {}, [], 0.0
    while ready:
        best = None
        for q, l in ready.items():
            f = free.get(q, 0.0) if q[1] else 0.0
            m = max(min(rt[k] for k in l), f)
            if best is None or m < best[0]:
                best = (m, q, f)
        m, q, f = best
        k0 = min([k for k in ready[q] if rt[k] <= m], key=key.get)
        look = 0.0 if q[1] in ("A", "B") else max(0.0, E["look"] * K[k0]["dur"] + prio.get((k0, "w"), 0.0))
        k1 = min([k for k in ready[q] if rt[k] <= m + look], key=key.get)
        ready[q].remove(k1)
        if not ready[q]:
            del ready[q]
        order.append(k1)
        e = max(rt[k1], f) + K[k1]["dur"]
        if q[1]:
            free[q] = e
        e += K[k1]["gap"]
        end = max(end, e)
        for c in kids[k1]:
            rt[c] = max(rt[c], e)
            left[c] -= 1
            if left[c] == 0:
                ready.setdefault((c[0], K[c]["q"]), []).append(c)
    return order, end


def replay(K, order):
    free, fin = {}, {}
    for k in order:
        t = K[k]
        st = max([fin[d] for d in t["deps"]] + [free.get((k[0], t["q"]), 0.0)])
        if t["q"]:
            free[(k[0], t["q"])] = st + t["dur"]
        fin[k] = st + t["dur"] + t["gap"]
    return max(fin.values()), fin


def search(E, tries, seed):
    K = tasks_of(E)
    KO = [tasks_of(dict(E, **o)) for o in OTHERS]
    names = [k for k in K if K[k]["do"] and K[k]["q"] in "vatg" and k[1][-2:-1] == "_"]
    rng = np.random.RandomState(seed)

    def cost(p):
        o, e = plan(K, E, p)
        return e + sum(replay(k2, o)[0] for k2 in KO), o
    prio = {}
    best, order = cost(prio)
    for it in range(tries):
        p = dict(prio)
        for j in range(int(rng.randint(1, 4))):
            k = names[int(rng.randint(len(names)))]
            z = rng.rand()
            if z < 0.3:
                dl = float(rng.randn() * 2.0)
                for k2 in names:
                    if k2[0] == k[0] and k2[1][-3:] == k[1][-3:]:
                        p[k2] = p.get(k2, 0.0) + dl
            elif z < 0.5:
                p[(k, "w")] = float(rng.rand() * 1.5 - 0.3)
            else:
                p[k] = p.get(k, 0.0) + float(rng.randn() * 3.0)
        c, o = cost(p)
        if c <= best:
            best, order, prio = c, o, p
    return K, order, best


MEMO = {}


def rank_program(g, core, T, topo):
    rank = T.rank_of(core)
    if rank is None:
        return
    if "plan" not in MEMO:
        MEMO["K"], MEMO["plan"], MEMO["cost"] = search(EST, TRIES, SEED)
    K = MEMO["K"]
    chips = []
    for c in T.cores:
        if topo.chip(c) not in chips:
            chips.append(topo.chip(c))
    pairs = [[c for c in T.cores if topo.chip(c) == ch] for ch in chips]
    mine = [p for p in pairs if core in p][0]
    side = mine.index(core)
    sib = mine[1 - side]
    moff = -1
    for c in T.cores:
        if c not in mine:
            moff &= topo.mask(core, c)
    mon = topo.mask(core, sib) & ~moff
    noff, non = bin(moff).count("1"), bin(mon).count("1")
    slot = pairs.index(mine)
    x = dict(g=g, T=T, topo=topo, pairs=pairs, sib=sib, moff=moff, mon=mon, noff=noff, non=non, sent=[0],
             rank=rank, slot=slot, d=(0.25 if slot == 0 else 0.5) / 32)
    QS = {"g": g, "v": g.vector, "a": g.scalar, "t": g.tensor, "s": g.sync}
    count = {q: 0 for q in CSEM}
    known = {q: {} for q in QS}
    done = {}
    outs = [0]
    for k in MEMO["plan"]:
        t = K[k]
        if k[0] != side:
            continue
        if t["sem"]:
            name, val = t["sem"]
            if val == "all":
                val = (len(T.cores) - 2) * noff + non
            elif val is None:
                val = (len(pairs) - 1) * noff + non if name.startswith("ha") else non
            done[k] = (name, val, {})
            continue
        if t["do"] is None:
            continue
        q = t["q"]
        need = {}
        for d in t["deps"]:
            if d[1] in t.get("same", ()):
                continue
            name, val, clock = done[d]
            if val > need.get(name, (0, None))[0]:
                need[name] = (val, clock)
        for name, (val, clock) in sorted(need.items(), key=lambda e: -len(e[1][1])):
            if known[q].get(name, 0) < val:
                QS[q].wait_ge(T.sem[name], val)
                known[q][name] = val
                for n2, v2 in clock.items():
                    known[q][n2] = max(known[q].get(n2, 0), v2)
        ins = t["do"](QS[q], T, x)
        if t.get("dma"):
            outs[0] += 16 if t.get("out") else 0
            continue
        for i in ins:
            i.then_inc(T.sem[CSEM[q]], 1)
        count[q] += len(ins)
        done[k] = (CSEM[q], count[q], dict(known[q]))
    for q in CSEM:
        g.wait_ge(T.sem[CSEM[q]], count[q])
    g.wait_ge(T.sem.lsent, x["sent"][0])
    g.sync.wait_ge(T.sem.outs, outs[0])
